import numpy as np
import ml_dtypes


def mxq(x, axis, fmt="e4m3"):
    dtype, down = {"e4m3": (ml_dtypes.float8_e4m3fn, 7), "e5m2": (ml_dtypes.float8_e5m2, 14)}[fmt]
    v = np.moveaxis(np.asarray(x, np.float32).astype(ml_dtypes.bfloat16).astype(np.float64), axis, -1)
    blocks = v.reshape(v.shape[:-1] + (-1, 32))
    amax = np.abs(blocks).max(-1, keepdims=True)
    byte = np.maximum(np.where(amax > 0, np.frexp(amax)[1] - 1 + 127, 0) - down, 1)
    scale = np.exp2(byte - 127.0)
    codes = (blocks / scale).astype(np.float32).astype(dtype).astype(np.float64)
    return np.moveaxis((codes * scale).reshape(v.shape), -1, axis)


WIDE = False


def mx_kscale(k):
    if not WIDE:
        return np.ones(k)
    levels = np.array([10, -10, 5, -5, 0])
    if k % 512:
        return np.exp2(np.random.permutation(np.resize(levels, k // 32))).repeat(32)
    a = np.empty((k // 512, 16))
    for p in range(k // 512):
        a[p, :8] = np.random.permutation(np.resize(levels, 8))
        for g in range(8):
            far = levels[np.abs(levels - a[p, g]) >= 10]
            a[p, g + 8] = far[np.random.randint(len(far))]
    return np.exp2(a.ravel()).repeat(32)


def f64(x):
    return np.asarray(x).astype(np.float64)


def striped(idx):
    return np.tile(idx.reshape(-1, 16).T, (8, 1)).astype(np.uint16)


def unstriped(offs):
    return offs[:16].T.reshape(-1).astype(np.int64)


E2M1 = np.array([0.0, 0.5, 1.0, 1.5, 2.0, 3.0, 4.0, 6.0, -0.0, -0.5, -1.0, -1.5, -2.0, -3.0, -4.0, -6.0])


def pack_weight(w, fmt):
    k, n = w.shape
    w = f64(np.asarray(w, np.float32).astype(ml_dtypes.bfloat16)).reshape(k // 32, 32, n)
    amax = np.abs(w).max(1)
    if fmt == "e4m3":
        byte = np.frexp(amax)[1] - 1 + 127 - 7
    else:
        mant, ex = np.frexp(amax / 6.0)
        byte = np.where(mant > 0.5, ex, ex - 1) + 127
    byte = np.clip(np.where(amax > 0, byte, 1), 1, 254)
    scaled = (w * np.exp2(127.0 - byte)[:, None, :]).reshape(k, n).astype(np.float32)
    by_word = np.ascontiguousarray(scaled.reshape(k // 512, 128, 4, n).transpose(0, 1, 3, 2))
    if fmt == "e4m3":
        words = by_word.astype(ml_dtypes.float8_e4m3fn).view(np.uint8)
    else:
        c = by_word.astype(ml_dtypes.float4_e2m1fn).view(np.uint8) & 0xF
        words = (c[..., 0::2] | (c[..., 1::2] << 4)).reshape(k // 512, 128, 2 * n)
    return np.ascontiguousarray(words), np.ascontiguousarray(byte.astype(np.uint8).reshape(k // 512, 16, n))


def unpack_weight(words, scales, fmt):
    g, _, n = scales.shape
    words = np.ascontiguousarray(words).reshape(g, 128, n, -1)
    if fmt == "e4m3":
        vals = words.view(ml_dtypes.float8_e4m3fn).astype(np.float64)
    else:
        nib = np.empty((g, 128, n, 4), np.uint8)
        nib[..., 0::2] = words & 0xF
        nib[..., 1::2] = words >> 4
        vals = E2M1[nib]
    vals = vals * np.repeat(np.exp2(scales.astype(np.float64) - 127.0), 8, axis=1)[..., None]
    return vals.transpose(0, 1, 3, 2).reshape(g * 512, n)


def sigmoid(v):
    return 1.0 / (1.0 + np.exp(-np.maximum(v, -700.0)))


K, T, E, C, H, N = 1024, 512, 6, 128, 512, 256
TOP = 4
PAD = 64


def by_expert(wq, xq):
    return np.concatenate([wq[e].T @ xq[:, e * C:(e + 1) * C] for e in range(E)], axis=1)


def setup_inputs():
    n = np.random.standard_normal
    s = mx_kscale(K)[:, None]
    u = mx_kscale(H)
    slot_token = np.empty(E * C, np.int64); pos = np.tile(E * C + np.arange(T) % PAD, (TOP, 1)); taken = np.zeros(T, np.int64)
    liked = np.random.randn(T)
    for e in np.random.permutation(E):
        free = np.flatnonzero(taken < TOP); pick = np.random.permutation(free[np.argsort(-(liked[free] + np.random.gumbel(size=free.size)))[:C]]); slot_token[e * C:(e + 1) * C] = pick
        pos[taken[pick], pick] = e * C + np.arange(C); taken[pick] += 1
    g = np.random.uniform(0.2, 0.8, (TOP, T))
    w1 = [pack_weight(m, "e2m1") for m in n((E, K, H)) / np.sqrt(K) / s[None]]
    w3 = [pack_weight(m, "e2m1") for m in n((E, K, H)) / np.sqrt(K) / s[None] * u[None, None, :]]
    w2 = [pack_weight(m, "e2m1") for m in n((E, H, N)) / np.sqrt(H) / u[None, :, None]]
    x = pack_weight(n((K, T)) * s, "e4m3")
    return {
        "x_words": x[0],
        "x_scales": x[1],
        "w1_words": np.stack([m[0] for m in w1]),
        "w1_scales": np.stack([m[1] for m in w1]),
        "w3_words": np.stack([m[0] for m in w3]),
        "w3_scales": np.stack([m[1] for m in w3]),
        "w2_words": np.stack([m[0] for m in w2]),
        "w2_scales": np.stack([m[1] for m in w2]),
        "gate": np.stack([np.tile(r, (N, 1)) for r in g]).astype(np.float32),
        "offs": striped(slot_token),
        "pos1": striped(pos[0]),
        "pos2": striped(pos[1]),
        "pos3": striped(pos[2]),
        "pos4": striped(pos[3]),
    }


def reference(x_words, x_scales, w1_words, w1_scales, w3_words, w3_scales, w2_words, w2_scales, gate, offs, pos1, pos2, pos3, pos4):
    idx = unstriped(offs)
    w1 = np.stack([unpack_weight(w1_words[e], w1_scales[e], "e2m1") for e in range(E)])
    w3 = np.stack([unpack_weight(w3_words[e], w3_scales[e], "e2m1") for e in range(E)])
    w2 = np.stack([unpack_weight(w2_words[e], w2_scales[e], "e2m1") for e in range(E)])
    xq = unpack_weight(x_words, x_scales, "e4m3")[:, idx]
    h = sigmoid(by_expert(w1, xq))
    h = h * by_expert(w3, xq)
    y = by_expert(w2, mxq(h, 0, "e4m3"))
    y = np.concatenate([y, np.zeros((N, PAD))], axis=1)
    return sum(f64(gate[r]) * y[:, unstriped(p)] for r, p in enumerate((pos1, pos2, pos3, pos4)))

@@ -1,0 +1,217 @@
+from contextlib import ExitStack
+
+import concourse.mybir as mybir
+from concourse.masks import make_identity
+
+K, T, E, C, H, N = 1024, 512, 6, 128, 512, 256
+TOP = 4
+PAD = 64
+SLOTS = E * C
+P = 128
+PASSES = K // 512
+HALVES = N // P
+
+FLOPS = 2 * SLOTS * (2 * K * H + H * N)
+
+F32 = mybir.dt.float32
+BF16 = mybir.dt.bfloat16
+I32 = mybir.dt.int32
+U32 = mybir.dt.uint32
+U16 = mybir.dt.uint16
+U8 = mybir.dt.uint8
+FP8X4 = mybir.dt.float8_e4m3fn_x4
+FP4X4 = mybir.dt.float4_e2m1fn_x4
+MULT = mybir.AluOpType.mult
+ADD = mybir.AluOpType.add
+SIGMOID = mybir.ActivationFunctionType.Sigmoid
+
+SCALE_GROUP = 2
+GATHER_GROUP = 2
+
+
+def load_scale_rows(nc, plane, rows):
+    for r in range(4):
+        nc.sync.dma_start(out=plane[r:P:32, :, :].bitcast(I32), in_=rows[r])
+
+
+def tile_moe_ecr_glu_sigmoid_kernel(
+    tc, x_words, x_scales, w1_words, w1_scales, w3_words, w3_scales, w2_words, w2_scales, gate, offs, pos1, pos2, pos3, pos4, out
+):
+    nc = tc.nc
+    with ExitStack() as ctx:
+        lists = ctx.enter_context(tc.tile_pool(name="lists", bufs=1))
+        keep = ctx.enter_context(tc.tile_pool(name="keep", bufs=1))
+        ring = ctx.enter_context(tc.tile_pool(name="ring", bufs=2))
+        psum_ab = ctx.enter_context(tc.psum_pool(name="psum_ab", bufs=6))
+        psum_t = ctx.enter_context(tc.psum_pool(name="psum_t", bufs=2))
+
+        offs_sb = lists.tile([P, SLOTS // 16], U16, name="offs_sb")
+        pos_sb = [lists.tile([P, T // 16], U16, name="pos_sb%d" % r) for r in range(TOP)]
+
+        x_win = keep.tile([P, PASSES, T], I32, name="x_win", align_bytes=64)
+        xs_win = keep.tile([P, PASSES, T], U8, name="xs_win", align_bytes=64)
+        groups = E // SCALE_GROUP
+        w1_plane = [keep.tile([P, SCALE_GROUP * PASSES, H], U8, name="w1_plane%d" % g, align_bytes=64) for g in range(groups)]
+        w3_plane = [keep.tile([P, SCALE_GROUP * PASSES, H], U8, name="w3_plane%d" % g, align_bytes=64) for g in range(groups)]
+        w2_plane = keep.tile([P, E, N], U8, name="w2_plane", align_bytes=64)
+        w1_sb = keep.tile([P, E * PASSES, 2 * H], U8, name="w1_sb", align_bytes=64)
+        w3_sb = keep.tile([P, E * PASSES, 2 * H], U8, name="w3_sb", align_bytes=64)
+        w2_sb = keep.tile([P, E, 2 * N], U8, name="w2_sb", align_bytes=64)
+        gate_sb = keep.tile([P, TOP, HALVES, T], F32, name="gate_sb")
+        y_win = [keep.tile([P, SLOTS + PAD], F32, name="y_win%d" % hf) for hf in range(HALVES)]
+        ident = keep.tile([P, P], F32, name="ident")
+
+        nc.vector.memset(xs_win[:].bitcast(I32), 0)
+        for g in range(groups):
+            nc.vector.memset(w1_plane[g][:].bitcast(I32), 0)
+            nc.vector.memset(w3_plane[g][:].bitcast(I32), 0)
+        nc.vector.memset(w2_plane[:].bitcast(I32), 0)
+        for hf in range(HALVES):
+            nc.vector.memset(y_win[hf][:, SLOTS:], 0.0)
+        make_identity(nc, ident[:])
+
+        nc.sync.dma_start(out=x_win[:], in_=x_words.rearrange("s p t r -> p s (t r)").bitcast(I32))
+        nc.sync.dma_start(offs_sb[:], offs)
+        load_scale_rows(nc, xs_win, x_scales.bitcast(I32).rearrange("s (q r) c -> r q s c", r=4))
+        w1_rows = w1_scales.bitcast(I32).rearrange("e s (q r) c -> r q (e s) c", r=4)
+        w3_rows = w3_scales.bitcast(I32).rearrange("e s (q r) c -> r q (e s) c", r=4)
+        w2_rows = w2_scales.bitcast(I32).rearrange("e s (q r) c -> r q (e s) c", r=4)
+        w1_all = w1_words.bitcast(I32).rearrange("e s p c -> p (e s) c")
+        w3_all = w3_words.bitcast(I32).rearrange("e s p c -> p (e s) c")
+        for g in range(groups):
+            planes = slice(g * SCALE_GROUP * PASSES, (g + 1) * SCALE_GROUP * PASSES)
+            load_scale_rows(nc, w1_plane[g], w1_rows[:, :, planes, :])
+            load_scale_rows(nc, w3_plane[g], w3_rows[:, :, planes, :])
+            step = SCALE_GROUP * PASSES if g < groups - 1 else PASSES
+            for first in range(planes.start, planes.stop, step):
+                part = slice(first, first + step)
+                nc.sync.dma_start(out=w1_sb[:, part, :].bitcast(I32), in_=w1_all[:, part, :])
+                nc.sync.dma_start(out=w3_sb[:, part, :].bitcast(I32), in_=w3_all[:, part, :])
+        load_scale_rows(nc, w2_plane, w2_rows)
+        nc.sync.dma_start(out=w2_sb[:].bitcast(I32), in_=w2_words.bitcast(I32).rearrange("e s p c -> p (e s) c"))
+        for r, pos in enumerate((pos1, pos2, pos3, pos4)):
+            nc.sync.dma_start(pos_sb[r][:], pos)
+        gate_rows = gate.rearrange("r (h p) t -> p r h t", p=P)
+        nc.sync.dma_start(out=gate_sb[:, 0, 0, :], in_=gate_rows[:, 0, 0, :])
+        nc.sync.dma_start(out=gate_sb[:, 1:3, 0, :], in_=gate_rows[:, 1:3, 0, :])
+        nc.sync.dma_start(out=gate_sb[:, 0:3, 1, :], in_=gate_rows[:, 0:3, 1, :])
+        nc.sync.dma_start(out=gate_sb[:, 3, :, :], in_=gate_rows[:, 3, :, :])
+
+        width = GATHER_GROUP * C
+        x_slot = []
+        xs_slot = []
+        for g in range(E // GATHER_GROUP):
+            picks = offs_sb[:, g * width // 16 : (g + 1) * width // 16]
+            x_slot.append([keep.tile([P, width], U32, name="x_slot%d_%d" % (g, s), align_bytes=64) for s in range(PASSES)])
+            xs_slot.append([keep.tile([P, width], U8, name="xs_slot%d_%d" % (g, s), align_bytes=64) for s in range(PASSES)])
+            for s in range(PASSES):
+                nc.vector.tensor_copy(out=x_slot[g][s][:], in_=x_win[:, s, :].bitcast(U32).indirect(picks))
+            for s in range(PASSES):
+                nc.vector.tensor_copy(out=xs_slot[g][s][:], in_=xs_win[:, s, :].indirect(picks))
+
+        h_codes = [keep.tile([P, C], U32, name="h_codes%d" % e, align_bytes=64) for e in range(E)]
+        h_scales = [keep.tile([P, C], U8, name="h_scales%d" % e, align_bytes=64) for e in range(E)]
+
+        def first_layer(e):
+            g, place = divmod(e, GATHER_GROUP)
+            cols = slice(place * C, (place + 1) * C)
+            sums = []
+            for w_sb, w_plane in ((w1_sb, w1_plane), (w3_sb, w3_plane)):
+                acc = psum_ab.tile([C, H], F32, name="acc", tag="acc")
+                for s in range(PASSES):
+                    nc.tensor.matmul_mx(
+                        out=acc[:],
+                        lhsT=x_slot[g][s][:, cols].bitcast(FP8X4),
+                        lhsT_scale=xs_slot[g][s][:, cols],
+                        rhs=w_sb[:, e * PASSES + s, :].bitcast(FP4X4),
+                        rhs_scale=w_plane[e // SCALE_GROUP][:, (e % SCALE_GROUP) * PASSES + s, :],
+                        start=(s == 0),
+                        stop=(s == PASSES - 1),
+                    )
+                sums.append(acc[:].rearrange("j (p u d) -> j u p d", u=2, d=2))
+            sig = ring.tile([C, 2, P, 2], F32, name="sig")
+            nc.scalar.activation(out=sig[:], in_=sums[0], func=SIGMOID)
+            h_rows = ring.tile([C, 2, P, 2], BF16, name="h_rows")
+            nc.vector.tensor_tensor(out=h_rows[:], in0=sig[:], in1=sums[1], op=MULT)
+            return h_rows
+
+        def turn_and_quantize(e, h_rows):
+            pairs = h_rows[:].rearrange("j u p d -> j (u p d)").bitcast(F32)
+            turned = psum_t.tile([P, 2, C], F32, name="turned")
+            for u in range(2):
+                nc.tensor.transpose(turned[:, u, :], pairs[:, u * P : (u + 1) * P], ident[:])
+            h_cols = ring.tile([P, 4 * C], BF16, name="h_cols", align_bytes=64)
+            nc.scalar.copy(
+                out=h_cols[:].bitcast(F32).rearrange("p (j u) -> p j u", u=2),
+                in_=turned[:].rearrange("p u j -> p j u"),
+            )
+            nc.vector.quantize_mx(out=h_codes[e][:].bitcast(FP8X4), scales=h_scales[e][:], in_=h_cols[:])
+
+        def second_product(e, hf, dst):
+            nc.tensor.matmul_mx(
+                out=dst,
+                lhsT=w2_sb[:, e, 2 * hf * P : 2 * (hf + 1) * P].bitcast(FP4X4),
+                lhsT_scale=w2_plane[:, e, hf * P : (hf + 1) * P],
+                rhs=h_codes[e][:].bitcast(FP8X4),
+                rhs_scale=h_scales[e][:],
+                start=True,
+                stop=True,
+            )
+
+        def second_layer_first_four():
+            for hf in range(HALVES):
+                y_acc = psum_ab.tile([P, 4 * C], F32, name="y_acc", tag="acc")
+                for e in range(4):
+                    second_product(e, hf, y_acc[:, e * C : (e + 1) * C])
+                nc.scalar.copy(out=y_win[hf][:, 0 : 4 * C], in_=y_acc[:])
+
+        def second_layer(e):
+            y_acc = psum_ab.tile([P, HALVES * C], F32, name="y_acc", tag="acc")
+            for hf in range(HALVES):
+                second_product(e, hf, y_acc[:, hf * C : (hf + 1) * C])
+            for hf in range(HALVES):
+                nc.scalar.copy(out=y_win[hf][:, e * C : (e + 1) * C], in_=y_acc[:, hf * C : (hf + 1) * C])
+
+        rows = {}
+        for e in range(E):
+            rows[e] = first_layer(e)
+            if e > 0:
+                turn_and_quantize(e - 1, rows[e - 1])
+        second_layer_first_four()
+        second_layer(4)
+        turn_and_quantize(E - 1, rows[E - 1])
+        second_layer(5)
+
+        prod = [[keep.tile([P, T], F32, name="prod%d_%d" % (hf, r)) for r in range(TOP)] for hf in range(HALVES)]
+        blocks = T // P
+
+        def fetch(hf, r):
+            nc.vector.tensor_tensor(out=prod[hf][r][:], in0=y_win[hf][:].indirect(pos_sb[r][:]), in1=gate_sb[:, r, hf, :], op=MULT)
+
+        back = []
+        for hf in range(HALVES):
+            sum_t = psum_ab.tile([P, T], F32, name="sum_t", tag="acc")
+            for r in range(TOP - 1):
+                fetch(hf, r)
+                for b in range(blocks):
+                    cols = slice(b * P, (b + 1) * P)
+                    nc.tensor.matmul(
+                        sum_t[:, cols],
+                        lhsT=prod[hf][r][:, cols],
+                        rhs=ident[:],
+                        is_transpose=True,
+                        start=(r == 0 and b == 0),
+                        stop=(r == TOP - 2 and b == blocks - 1),
+                    )
+            sum_sb = ring.tile([P, T], F32, name="sum_sb")
+            nc.scalar.copy(out=sum_sb[:], in_=sum_t[:])
+            back.append(psum_ab.tile([P, T], F32, name="back", tag="acc"))
+            for b in range(blocks):
+                cols = slice(b * P, (b + 1) * P)
+                nc.tensor.transpose(back[hf][:, cols], sum_sb[:, cols], ident[:])
+        for hf in range(HALVES):
+            fetch(hf, TOP - 1)
+        for hf, cols in ((0, slice(0, T)), (1, slice(0, T // 2)), (1, slice(T // 2, T))):
+            result = keep.tile([P, cols.stop - cols.start], F32, name="result%d_%d" % (hf, cols.start))
+            nc.vector.tensor_tensor(out=result[:], in0=prod[hf][TOP - 1][:, cols], in1=back[hf][:, cols], op=ADD)
+            nc.sync.dma_start(out=out[hf * P : (hf + 1) * P, cols], in_=result[:])

@@ -25,7 +25,7 @@ MULT = mybir.AluOpType.mult
 ADD = mybir.AluOpType.add
 SIGMOID = mybir.ActivationFunctionType.Sigmoid
 
-SCALE_GROUP = 2
+SCALE_GROUPS = ((0, 1), (2, 3, 4, 5))
 GATHER_GROUP = 2
 
 
@@ -50,19 +50,18 @@ def tile_moe_ecr_glu_sigmoid_kernel(
 
         x_win = keep.tile([P, PASSES, T], I32, name="x_win", align_bytes=64)
         xs_win = keep.tile([P, PASSES, T], U8, name="xs_win", align_bytes=64)
-        groups = E // SCALE_GROUP
-        w1_plane = [keep.tile([P, SCALE_GROUP * PASSES, H], U8, name="w1_plane%d" % g, align_bytes=64) for g in range(groups)]
-        w3_plane = [keep.tile([P, SCALE_GROUP * PASSES, H], U8, name="w3_plane%d" % g, align_bytes=64) for g in range(groups)]
+        w1_plane = [keep.tile([P, len(g) * PASSES, H], U8, name="w1_plane%d" % g[0], align_bytes=64) for g in SCALE_GROUPS]
+        w3_plane = [keep.tile([P, len(g) * PASSES, H], U8, name="w3_plane%d" % g[0], align_bytes=64) for g in SCALE_GROUPS]
         w2_plane = keep.tile([P, E, N], U8, name="w2_plane", align_bytes=64)
         w1_sb = keep.tile([P, E * PASSES, 2 * H], U8, name="w1_sb", align_bytes=64)
         w3_sb = keep.tile([P, E * PASSES, 2 * H], U8, name="w3_sb", align_bytes=64)
         w2_sb = keep.tile([P, E, 2 * N], U8, name="w2_sb", align_bytes=64)
-        gate_sb = keep.tile([P, TOP, HALVES, T], F32, name="gate_sb")
+        gate_sb = [keep.tile([P, T], F32, name="gate_sb%d" % r) for r in range(TOP)]
         y_win = [keep.tile([P, SLOTS + PAD], F32, name="y_win%d" % hf) for hf in range(HALVES)]
         ident = keep.tile([P, P], F32, name="ident")
 
         nc.vector.memset(xs_win[:].bitcast(I32), 0)
-        for g in range(groups):
+        for g in range(len(SCALE_GROUPS)):
             nc.vector.memset(w1_plane[g][:].bitcast(I32), 0)
             nc.vector.memset(w3_plane[g][:].bitcast(I32), 0)
         nc.vector.memset(w2_plane[:].bitcast(I32), 0)
@@ -70,32 +69,36 @@ def tile_moe_ecr_glu_sigmoid_kernel(
             nc.vector.memset(y_win[hf][:, SLOTS:], 0.0)
         make_identity(nc, ident[:])
 
-        nc.sync.dma_start(out=x_win[:], in_=x_words.rearrange("s p t r -> p s (t r)").bitcast(I32))
-        nc.sync.dma_start(offs_sb[:], offs)
-        load_scale_rows(nc, xs_win, x_scales.bitcast(I32).rearrange("s (q r) c -> r q s c", r=4))
         w1_rows = w1_scales.bitcast(I32).rearrange("e s (q r) c -> r q (e s) c", r=4)
         w3_rows = w3_scales.bitcast(I32).rearrange("e s (q r) c -> r q (e s) c", r=4)
         w2_rows = w2_scales.bitcast(I32).rearrange("e s (q r) c -> r q (e s) c", r=4)
         w1_all = w1_words.bitcast(I32).rearrange("e s p c -> p (e s) c")
         w3_all = w3_words.bitcast(I32).rearrange("e s p c -> p (e s) c")
-        for g in range(groups):
-            planes = slice(g * SCALE_GROUP * PASSES, (g + 1) * SCALE_GROUP * PASSES)
-            load_scale_rows(nc, w1_plane[g], w1_rows[:, :, planes, :])
-            load_scale_rows(nc, w3_plane[g], w3_rows[:, :, planes, :])
-            step = SCALE_GROUP * PASSES if g < groups - 1 else PASSES
-            for first in range(planes.start, planes.stop, step):
-                part = slice(first, first + step)
-                nc.sync.dma_start(out=w1_sb[:, part, :].bitcast(I32), in_=w1_all[:, part, :])
-                nc.sync.dma_start(out=w3_sb[:, part, :].bitcast(I32), in_=w3_all[:, part, :])
-        load_scale_rows(nc, w2_plane, w2_rows)
-        nc.sync.dma_start(out=w2_sb[:].bitcast(I32), in_=w2_words.bitcast(I32).rearrange("e s p c -> p (e s) c"))
+
+        def load_words(w_sb, w_all, first, last):
+            part = slice(first * PASSES, (last + 1) * PASSES)
+            nc.sync.dma_start(out=w_sb[:, part, :].bitcast(I32), in_=w_all[:, part, :])
+
+        def load_group(g, w_plane, w_rows, w_sb, w_all):
+            experts = SCALE_GROUPS[g]
+            load_scale_rows(nc, w_plane[g], w_rows[:, :, experts[0] * PASSES : (experts[-1] + 1) * PASSES, :])
+            load_words(w_sb, w_all, experts[0], experts[1])
+
+        nc.sync.dma_start(out=x_win[:], in_=x_words.rearrange("s p t r -> p s (t r)").bitcast(I32))
+        load_scale_rows(nc, xs_win, x_scales.bitcast(I32).rearrange("s (q r) c -> r q s c", r=4))
+        nc.sync.dma_start(offs_sb[:], offs)
+        for g in range(len(SCALE_GROUPS)):
+            load_group(g, w1_plane, w1_rows, w1_sb, w1_all)
+            load_group(g, w3_plane, w3_rows, w3_sb, w3_all)
         for r, pos in enumerate((pos1, pos2, pos3, pos4)):
             nc.sync.dma_start(pos_sb[r][:], pos)
-        gate_rows = gate.rearrange("r (h p) t -> p r h t", p=P)
-        nc.sync.dma_start(out=gate_sb[:, 0, 0, :], in_=gate_rows[:, 0, 0, :])
-        nc.sync.dma_start(out=gate_sb[:, 1:3, 0, :], in_=gate_rows[:, 1:3, 0, :])
-        nc.sync.dma_start(out=gate_sb[:, 0:3, 1, :], in_=gate_rows[:, 0:3, 1, :])
-        nc.sync.dma_start(out=gate_sb[:, 3, :, :], in_=gate_rows[:, 3, :, :])
+        for e in (4, 5):
+            load_words(w1_sb, w1_all, e, e)
+            load_words(w3_sb, w3_all, e, e)
+        load_scale_rows(nc, w2_plane, w2_rows)
+        nc.sync.dma_start(out=w2_sb[:].bitcast(I32), in_=w2_words.bitcast(I32).rearrange("e s p c -> p (e s) c"))
+        for r in range(TOP):
+            nc.sync.dma_start(out=gate_sb[r][:], in_=gate[r, 0:P, :])
 
         width = GATHER_GROUP * C
         x_slot = []
@@ -115,6 +118,7 @@ def tile_moe_ecr_glu_sigmoid_kernel(
         def first_layer(e):
             g, place = divmod(e, GATHER_GROUP)
             cols = slice(place * C, (place + 1) * C)
+            sg = 0 if e in SCALE_GROUPS[0] else 1
             sums = []
             for w_sb, w_plane in ((w1_sb, w1_plane), (w3_sb, w3_plane)):
                 acc = psum_ab.tile([C, H], F32, name="acc", tag="acc")
@@ -124,7 +128,7 @@ def tile_moe_ecr_glu_sigmoid_kernel(
                         lhsT=x_slot[g][s][:, cols].bitcast(FP8X4),
                         lhsT_scale=xs_slot[g][s][:, cols],
                         rhs=w_sb[:, e * PASSES + s, :].bitcast(FP4X4),
-                        rhs_scale=w_plane[e // SCALE_GROUP][:, (e % SCALE_GROUP) * PASSES + s, :],
+                        rhs_scale=w_plane[sg][:, (e - SCALE_GROUPS[sg][0]) * PASSES + s, :],
                         start=(s == 0),
                         stop=(s == PASSES - 1),
                     )
@@ -186,7 +190,7 @@ def tile_moe_ecr_glu_sigmoid_kernel(
         blocks = T // P
 
         def fetch(hf, r):
-            nc.vector.tensor_tensor(out=prod[hf][r][:], in0=y_win[hf][:].indirect(pos_sb[r][:]), in1=gate_sb[:, r, hf, :], op=MULT)
+            nc.vector.tensor_tensor(out=prod[hf][r][:], in0=y_win[hf][:].indirect(pos_sb[r][:]), in1=gate_sb[r][:], op=MULT)
 
         back = []
         for hf in range(HALVES):

@@ -27,6 +27,9 @@ SIGMOID = mybir.ActivationFunctionType.Sigmoid
 
 SCALE_GROUPS = ((0, 1), (2, 3, 4, 5))
 GATHER_GROUP = 2
+ROW_WORDS = H // 4
+W13_COLS = E * PASSES * ROW_WORDS
+STAGE_COLS = 2 * W13_COLS
 
 
 def load_scale_rows(nc, plane, rows):
@@ -50,8 +53,8 @@ def tile_moe_ecr_glu_sigmoid_kernel(
 
         x_win = keep.tile([P, PASSES, T], I32, name="x_win", align_bytes=64)
         xs_win = keep.tile([P, PASSES, T], U8, name="xs_win", align_bytes=64)
-        w1_plane = [keep.tile([P, len(g) * PASSES, H], U8, name="w1_plane%d" % g[0], align_bytes=64) for g in SCALE_GROUPS]
-        w3_plane = [keep.tile([P, len(g) * PASSES, H], U8, name="w3_plane%d" % g[0], align_bytes=64) for g in SCALE_GROUPS]
+        stage = keep.tile([P, STAGE_COLS], I32, name="stage", align_bytes=64)
+        w13_plane = [keep.tile([P, 2, len(g) * PASSES, H], U8, name="w13_plane%d" % g[0], align_bytes=64) for g in SCALE_GROUPS]
         w2_plane = keep.tile([P, E, N], U8, name="w2_plane", align_bytes=64)
         w1_sb = keep.tile([P, E * PASSES, 2 * H], U8, name="w1_sb", align_bytes=64)
         w3_sb = keep.tile([P, E * PASSES, 2 * H], U8, name="w3_sb", align_bytes=64)
@@ -62,15 +65,12 @@ def tile_moe_ecr_glu_sigmoid_kernel(
 
         nc.vector.memset(xs_win[:].bitcast(I32), 0)
         for g in range(len(SCALE_GROUPS)):
-            nc.vector.memset(w1_plane[g][:].bitcast(I32), 0)
-            nc.vector.memset(w3_plane[g][:].bitcast(I32), 0)
+            nc.vector.memset(w13_plane[g][:].bitcast(I32), 0)
         nc.vector.memset(w2_plane[:].bitcast(I32), 0)
         for hf in range(HALVES):
             nc.vector.memset(y_win[hf][:, SLOTS:], 0.0)
         make_identity(nc, ident[:])
 
-        w1_rows = w1_scales.bitcast(I32).rearrange("e s (q r) c -> r q (e s) c", r=4)
-        w3_rows = w3_scales.bitcast(I32).rearrange("e s (q r) c -> r q (e s) c", r=4)
         w2_rows = w2_scales.bitcast(I32).rearrange("e s (q r) c -> r q (e s) c", r=4)
         w1_all = w1_words.bitcast(I32).rearrange("e s p c -> p (e s) c")
         w3_all = w3_words.bitcast(I32).rearrange("e s p c -> p (e s) c")
@@ -79,17 +79,27 @@ def tile_moe_ecr_glu_sigmoid_kernel(
             part = slice(first * PASSES, (last + 1) * PASSES)
             nc.sync.dma_start(out=w_sb[:, part, :].bitcast(I32), in_=w_all[:, part, :])
 
-        def load_group(g, w_plane, w_rows, w_sb, w_all):
+        def move_scale_rows(g):
             experts = SCALE_GROUPS[g]
-            load_scale_rows(nc, w_plane[g], w_rows[:, :, experts[0] * PASSES : (experts[-1] + 1) * PASSES, :])
-            load_words(w_sb, w_all, experts[0], experts[1])
+            cols = slice(experts[0] * PASSES * ROW_WORDS, (experts[-1] + 1) * PASSES * ROW_WORDS)
+            for r in range(4):
+                nc.sync.dma_start(
+                    out=w13_plane[g][r:P:32].rearrange("p m a c -> p m (a c)").bitcast(I32),
+                    in_=stage[4 + 8 * r : P : 32, :].rearrange("p (m c) -> p m c", m=2)[:, :, cols],
+                )
 
+        for m, scales in enumerate((w1_scales, w3_scales)):
+            nc.sync.dma_start(
+                out=stage[4:P:8, m * W13_COLS : (m + 1) * W13_COLS].rearrange("q (a c) -> q a c", c=ROW_WORDS),
+                in_=scales.bitcast(I32).rearrange("e s q c -> q (e s) c"),
+            )
         nc.sync.dma_start(out=x_win[:], in_=x_words.rearrange("s p t r -> p s (t r)").bitcast(I32))
         load_scale_rows(nc, xs_win, x_scales.bitcast(I32).rearrange("s (q r) c -> r q s c", r=4))
         nc.sync.dma_start(offs_sb[:], offs)
         for g in range(len(SCALE_GROUPS)):
-            load_group(g, w1_plane, w1_rows, w1_sb, w1_all)
-            load_group(g, w3_plane, w3_rows, w3_sb, w3_all)
+            move_scale_rows(g)
+            load_words(w1_sb, w1_all, 2 * g, 2 * g + 1)
+            load_words(w3_sb, w3_all, 2 * g, 2 * g + 1)
         for r, pos in enumerate((pos1, pos2, pos3, pos4)):
             nc.sync.dma_start(pos_sb[r][:], pos)
         for e in (4, 5):
@@ -120,7 +130,7 @@ def tile_moe_ecr_glu_sigmoid_kernel(
             cols = slice(place * C, (place + 1) * C)
             sg = 0 if e in SCALE_GROUPS[0] else 1
             sums = []
-            for w_sb, w_plane in ((w1_sb, w1_plane), (w3_sb, w3_plane)):
+            for m, w_sb in enumerate((w1_sb, w3_sb)):
                 acc = psum_ab.tile([C, H], F32, name="acc", tag="acc")
                 for s in range(PASSES):
                     nc.tensor.matmul_mx(
@@ -128,7 +138,7 @@ def tile_moe_ecr_glu_sigmoid_kernel(
                         lhsT=x_slot[g][s][:, cols].bitcast(FP8X4),
                         lhsT_scale=xs_slot[g][s][:, cols],
                         rhs=w_sb[:, e * PASSES + s, :].bitcast(FP4X4),
-                        rhs_scale=w_plane[sg][:, (e - SCALE_GROUPS[sg][0]) * PASSES + s, :],
+                        rhs_scale=w13_plane[sg][:, m, (e - SCALE_GROUPS[sg][0]) * PASSES + s, :],
                         start=(s == 0),
                         stop=(s == PASSES - 1),
                     )

@@ -25,7 +25,7 @@ MULT = mybir.AluOpType.mult
 ADD = mybir.AluOpType.add
 SIGMOID = mybir.ActivationFunctionType.Sigmoid
 
-SCALE_GROUPS = ((0, 1), (2, 3, 4, 5))
+SCALE_GROUPS = ((0, 1), (2, 3), (4, 5))
 GATHER_GROUP = 2
 ROW_WORDS = H // 4
 W13_COLS = E * PASSES * ROW_WORDS
@@ -45,8 +45,8 @@ def tile_moe_ecr_glu_sigmoid_kernel(
         lists = ctx.enter_context(tc.tile_pool(name="lists", bufs=1))
         keep = ctx.enter_context(tc.tile_pool(name="keep", bufs=1))
         ring = ctx.enter_context(tc.tile_pool(name="ring", bufs=2))
-        psum_ab = ctx.enter_context(tc.psum_pool(name="psum_ab", bufs=6))
-        psum_t = ctx.enter_context(tc.psum_pool(name="psum_t", bufs=2))
+        psum = ctx.enter_context(tc.psum_pool(name="psum", bufs=1))
+        bank = [psum.tile([P, 512], F32, name="bank%d" % b) for b in range(8)]
 
         offs_sb = lists.tile([P, SLOTS // 16], U16, name="offs_sb")
         pos_sb = [lists.tile([P, T // 16], U16, name="pos_sb%d" % r) for r in range(TOP)]
@@ -56,8 +56,8 @@ def tile_moe_ecr_glu_sigmoid_kernel(
         stage = keep.tile([P, STAGE_COLS], I32, name="stage", align_bytes=64)
         w13_plane = [keep.tile([P, 2, len(g) * PASSES, H], U8, name="w13_plane%d" % g[0], align_bytes=64) for g in SCALE_GROUPS]
         w2_plane = keep.tile([P, E, N], U8, name="w2_plane", align_bytes=64)
-        w1_sb = keep.tile([P, E * PASSES, 2 * H], U8, name="w1_sb", align_bytes=64)
-        w3_sb = keep.tile([P, E * PASSES, 2 * H], U8, name="w3_sb", align_bytes=64)
+        w1_sb = [keep.tile([P, PASSES, 2 * H], U8, name="w1_sb%d" % e, tag="w1_sb%d" % e, align_bytes=64) for e in range(E)]
+        w3_sb = [keep.tile([P, PASSES, 2 * H], U8, name="w3_sb%d" % e, align_bytes=64) for e in range(E)]
         w2_sb = keep.tile([P, E, 2 * N], U8, name="w2_sb", align_bytes=64)
         gate_sb = [keep.tile([P, T], F32, name="gate_sb%d" % r) for r in range(TOP)]
         y_win = [keep.tile([P, SLOTS + PAD], F32, name="y_win%d" % hf) for hf in range(HALVES)]
@@ -66,18 +66,18 @@ def tile_moe_ecr_glu_sigmoid_kernel(
         nc.vector.memset(xs_win[:].bitcast(I32), 0)
         for g in range(len(SCALE_GROUPS)):
             nc.vector.memset(w13_plane[g][:].bitcast(I32), 0)
-        nc.vector.memset(w2_plane[:].bitcast(I32), 0)
+        nc.gpsimd.memset(w2_plane[:].bitcast(I32), 0)
         for hf in range(HALVES):
-            nc.vector.memset(y_win[hf][:, SLOTS:], 0.0)
+            nc.gpsimd.memset(y_win[hf][:, SLOTS:], 0.0)
         make_identity(nc, ident[:])
 
         w2_rows = w2_scales.bitcast(I32).rearrange("e s (q r) c -> r q (e s) c", r=4)
         w1_all = w1_words.bitcast(I32).rearrange("e s p c -> p (e s) c")
         w3_all = w3_words.bitcast(I32).rearrange("e s p c -> p (e s) c")
 
-        def load_words(w_sb, w_all, first, last):
-            part = slice(first * PASSES, (last + 1) * PASSES)
-            nc.sync.dma_start(out=w_sb[:, part, :].bitcast(I32), in_=w_all[:, part, :])
+        def load_words(e):
+            for w_sb, w_all in ((w1_sb, w1_all), (w3_sb, w3_all)):
+                nc.sync.dma_start(out=w_sb[e][:].bitcast(I32), in_=w_all[:, e * PASSES : (e + 1) * PASSES, :])
 
         def move_scale_rows(g):
             experts = SCALE_GROUPS[g]
@@ -88,35 +88,42 @@ def tile_moe_ecr_glu_sigmoid_kernel(
                     in_=stage[4 + 8 * r : P : 32, :].rearrange("p (m c) -> p m c", m=2)[:, :, cols],
                 )
 
+        nc.sync.dma_start(out=x_win[:], in_=x_words.rearrange("s p t r -> p s (t r)").bitcast(I32))
+        load_scale_rows(nc, xs_win, x_scales.bitcast(I32).rearrange("s (q r) c -> r q s c", r=4))
+        nc.sync.dma_start(offs_sb[:], offs)
         for m, scales in enumerate((w1_scales, w3_scales)):
             nc.sync.dma_start(
                 out=stage[4:P:8, m * W13_COLS : (m + 1) * W13_COLS].rearrange("q (a c) -> q a c", c=ROW_WORDS),
                 in_=scales.bitcast(I32).rearrange("e s q c -> q (e s) c"),
             )
-        nc.sync.dma_start(out=x_win[:], in_=x_words.rearrange("s p t r -> p s (t r)").bitcast(I32))
-        load_scale_rows(nc, xs_win, x_scales.bitcast(I32).rearrange("s (q r) c -> r q s c", r=4))
-        nc.sync.dma_start(offs_sb[:], offs)
-        for g in range(len(SCALE_GROUPS)):
-            move_scale_rows(g)
-            load_words(w1_sb, w1_all, 2 * g, 2 * g + 1)
-            load_words(w3_sb, w3_all, 2 * g, 2 * g + 1)
-        for r, pos in enumerate((pos1, pos2, pos3, pos4)):
-            nc.sync.dma_start(pos_sb[r][:], pos)
-        for e in (4, 5):
-            load_words(w1_sb, w1_all, e, e)
-            load_words(w3_sb, w3_all, e, e)
+
+        load_words(0)
+        nc.sync.dma_start(pos_sb[0][:], pos1)
+        nc.sync.dma_start(pos_sb[1][:], pos2)
+        move_scale_rows(0)
+        load_words(1)
+        move_scale_rows(1)
+        load_words(2)
+        load_words(3)
+        move_scale_rows(2)
+        nc.sync.dma_start(pos_sb[2][:], pos3)
+        nc.sync.dma_start(pos_sb[3][:], pos4)
+        load_words(4)
+        load_words(5)
         load_scale_rows(nc, w2_plane, w2_rows)
         nc.sync.dma_start(out=w2_sb[:].bitcast(I32), in_=w2_words.bitcast(I32).rearrange("e s p c -> p (e s) c"))
         for r in range(TOP):
             nc.sync.dma_start(out=gate_sb[r][:], in_=gate[r, 0:P, :])
 
         width = GATHER_GROUP * C
-        x_slot = []
-        xs_slot = []
-        for g in range(E // GATHER_GROUP):
+        x_slot = {}
+        xs_slot = {}
+
+        def gather_tokens(g):
             picks = offs_sb[:, g * width // 16 : (g + 1) * width // 16]
-            x_slot.append([keep.tile([P, width], U32, name="x_slot%d_%d" % (g, s), align_bytes=64) for s in range(PASSES)])
-            xs_slot.append([keep.tile([P, width], U8, name="xs_slot%d_%d" % (g, s), align_bytes=64) for s in range(PASSES)])
+            last = g == E // GATHER_GROUP - 1
+            x_slot[g] = [keep.tile([P, width], U32, name="x_slot%d_%d" % (g, s), tag=("sig%d" if last else "x_slot%d_%%d" % g) % s, align_bytes=64) for s in range(PASSES)]
+            xs_slot[g] = [keep.tile([P, width], U8, name="xs_slot%d_%d" % (g, s), tag=("h_rows0", "h_cols0")[s] if last else "xs_slot%d_%d" % (g, s), align_bytes=64) for s in range(PASSES)]
             for s in range(PASSES):
                 nc.vector.tensor_copy(out=x_slot[g][s][:], in_=x_win[:, s, :].bitcast(U32).indirect(picks))
             for s in range(PASSES):
@@ -128,36 +135,39 @@ def tile_moe_ecr_glu_sigmoid_kernel(
         def first_layer(e):
             g, place = divmod(e, GATHER_GROUP)
             cols = slice(place * C, (place + 1) * C)
-            sg = 0 if e in SCALE_GROUPS[0] else 1
+            sg = e // 2
             sums = []
             for m, w_sb in enumerate((w1_sb, w3_sb)):
-                acc = psum_ab.tile([C, H], F32, name="acc", tag="acc")
+                acc = bank[3 * m + e % 3]
                 for s in range(PASSES):
                     nc.tensor.matmul_mx(
                         out=acc[:],
                         lhsT=x_slot[g][s][:, cols].bitcast(FP8X4),
                         lhsT_scale=xs_slot[g][s][:, cols],
-                        rhs=w_sb[:, e * PASSES + s, :].bitcast(FP4X4),
+                        rhs=w_sb[e][:, s, :].bitcast(FP4X4),
                         rhs_scale=w13_plane[sg][:, m, (e - SCALE_GROUPS[sg][0]) * PASSES + s, :],
                         start=(s == 0),
                         stop=(s == PASSES - 1),
                     )
                 sums.append(acc[:].rearrange("j (p u d) -> j u p d", u=2, d=2))
-            sig = ring.tile([C, 2, P, 2], F32, name="sig")
+            sig = keep.tile([C, 2, P, 2], F32, name="sig%d" % e, tag="sig%d" % e, align_bytes=64)
             nc.scalar.activation(out=sig[:], in_=sums[0], func=SIGMOID)
-            h_rows = ring.tile([C, 2, P, 2], BF16, name="h_rows")
-            nc.vector.tensor_tensor(out=h_rows[:], in0=sig[:], in1=sums[1], op=MULT)
+            return sig, sums[1]
+
+        def gated_product(e, sig, b_sum):
+            h_rows = keep.tile([C, 2, P, 2], BF16, name="h_rows%d" % e, tag="h_rows%d" % e, align_bytes=64)
+            nc.vector.tensor_tensor(out=h_rows[:], in0=sig[:], in1=b_sum, op=MULT)
             return h_rows
 
         def turn_and_quantize(e, h_rows):
             pairs = h_rows[:].rearrange("j u p d -> j (u p d)").bitcast(F32)
-            turned = psum_t.tile([P, 2, C], F32, name="turned")
+            turned = bank[6 + e % 2][:, 0 : 2 * C].rearrange("p (u j) -> p u j", u=2)
             for u in range(2):
                 nc.tensor.transpose(turned[:, u, :], pairs[:, u * P : (u + 1) * P], ident[:])
-            h_cols = ring.tile([P, 4 * C], BF16, name="h_cols", align_bytes=64)
+            h_cols = keep.tile([P, 4 * C], BF16, name="h_cols%d" % e, tag="h_cols%d" % e, align_bytes=64)
             nc.scalar.copy(
                 out=h_cols[:].bitcast(F32).rearrange("p (j u) -> p j u", u=2),
-                in_=turned[:].rearrange("p u j -> p j u"),
+                in_=turned.rearrange("p u j -> p j u"),
             )
             nc.vector.quantize_mx(out=h_codes[e][:].bitcast(FP8X4), scales=h_scales[e][:], in_=h_cols[:])
 
@@ -174,26 +184,32 @@ def tile_moe_ecr_glu_sigmoid_kernel(
 
         def second_layer_first_four():
             for hf in range(HALVES):
-                y_acc = psum_ab.tile([P, 4 * C], F32, name="y_acc", tag="acc")
+                y_acc = bank[3 if hf == 0 else 0]
                 for e in range(4):
                     second_product(e, hf, y_acc[:, e * C : (e + 1) * C])
                 nc.scalar.copy(out=y_win[hf][:, 0 : 4 * C], in_=y_acc[:])
 
         def second_layer(e):
-            y_acc = psum_ab.tile([P, HALVES * C], F32, name="y_acc", tag="acc")
+            y_acc = bank[4 if e == 4 else 1]
             for hf in range(HALVES):
                 second_product(e, hf, y_acc[:, hf * C : (hf + 1) * C])
             for hf in range(HALVES):
                 nc.scalar.copy(out=y_win[hf][:, e * C : (e + 1) * C], in_=y_acc[:, hf * C : (hf + 1) * C])
 
         rows = {}
-        for e in range(E):
-            rows[e] = first_layer(e)
+        gather_tokens(0)
+        gather_tokens(1)
+        parts = {}
+        for e in range(E + 1):
+            if e < E:
+                parts[e] = first_layer(e)
             if e > 0:
+                rows[e - 1] = gated_product(e - 1, *parts[e - 1])
                 turn_and_quantize(e - 1, rows[e - 1])
+            if e == 2:
+                gather_tokens(2)
         second_layer_first_four()
         second_layer(4)
-        turn_and_quantize(E - 1, rows[E - 1])
         second_layer(5)
 
         prod = [[keep.tile([P, T], F32, name="prod%d_%d" % (hf, r)) for r in range(TOP)] for hf in range(HALVES)]
@@ -204,7 +220,7 @@ def tile_moe_ecr_glu_sigmoid_kernel(
 
         back = []
         for hf in range(HALVES):
-            sum_t = psum_ab.tile([P, T], F32, name="sum_t", tag="acc")
+            sum_t = bank[2 + 4 * hf]
             for r in range(TOP - 1):
                 fetch(hf, r)
                 for b in range(blocks):
@@ -219,7 +235,7 @@ def tile_moe_ecr_glu_sigmoid_kernel(
                     )
             sum_sb = ring.tile([P, T], F32, name="sum_sb")
             nc.scalar.copy(out=sum_sb[:], in_=sum_t[:])
-            back.append(psum_ab.tile([P, T], F32, name="back", tag="acc"))
+            back.append(bank[5 + 2 * hf])
             for b in range(blocks):
                 cols = slice(b * P, (b + 1) * P)
                 nc.tensor.transpose(back[hf][:, cols], sum_sb[:, cols], ident[:])

@@ -106,11 +106,11 @@ def tile_moe_ecr_glu_sigmoid_kernel(
         load_words(2)
         load_words(3)
         move_scale_rows(2)
+        load_scale_rows(nc, w2_plane, w2_rows)
         nc.sync.dma_start(pos_sb[2][:], pos3)
         nc.sync.dma_start(pos_sb[3][:], pos4)
         load_words(4)
         load_words(5)
-        load_scale_rows(nc, w2_plane, w2_rows)
         nc.sync.dma_start(out=w2_sb[:].bitcast(I32), in_=w2_words.bitcast(I32).rearrange("e s p c -> p (e s) c"))
         for r in range(TOP):
             nc.sync.dma_start(out=gate_sb[r][:], in_=gate[r, 0:P, :])
@@ -122,15 +122,15 @@ def tile_moe_ecr_glu_sigmoid_kernel(
         def gather_tokens(g):
             picks = offs_sb[:, g * width // 16 : (g + 1) * width // 16]
             last = g == E // GATHER_GROUP - 1
-            x_slot[g] = [keep.tile([P, width], U32, name="x_slot%d_%d" % (g, s), tag=("sig%d" if last else "x_slot%d_%%d" % g) % s, align_bytes=64) for s in range(PASSES)]
-            xs_slot[g] = [keep.tile([P, width], U8, name="xs_slot%d_%d" % (g, s), tag=("h_rows0", "h_cols0")[s] if last else "xs_slot%d_%d" % (g, s), align_bytes=64) for s in range(PASSES)]
+            x_slot[g] = [keep.tile([P, width], U32, name="x_slot%d_%d" % (g, s), tag="x_slot%d_%d" % (g, s), align_bytes=64) for s in range(PASSES)]
+            xs_slot[g] = [keep.tile([P, width], U8, name="xs_slot%d_%d" % (g, s), tag="sig%d" % s if last else "xs_slot%d_%d" % (g, s), align_bytes=64) for s in range(PASSES)]
             for s in range(PASSES):
                 nc.vector.tensor_copy(out=x_slot[g][s][:], in_=x_win[:, s, :].bitcast(U32).indirect(picks))
             for s in range(PASSES):
                 nc.vector.tensor_copy(out=xs_slot[g][s][:], in_=xs_win[:, s, :].indirect(picks))
 
-        h_codes = [keep.tile([P, C], U32, name="h_codes%d" % e, align_bytes=64) for e in range(E)]
-        h_scales = [keep.tile([P, C], U8, name="h_scales%d" % e, align_bytes=64) for e in range(E)]
+        h_codes = {}
+        h_scales = {}
 
         def first_layer(e):
             g, place = divmod(e, GATHER_GROUP)
@@ -159,42 +159,40 @@ def tile_moe_ecr_glu_sigmoid_kernel(
             nc.vector.tensor_tensor(out=h_rows[:], in0=sig[:], in1=b_sum, op=MULT)
             return h_rows
 
-        def turn_and_quantize(e, h_rows):
-            pairs = h_rows[:].rearrange("j u p d -> j (u p d)").bitcast(F32)
-            turned = bank[6 + e % 2][:, 0 : 2 * C].rearrange("p (u j) -> p u j", u=2)
-            for u in range(2):
-                nc.tensor.transpose(turned[:, u, :], pairs[:, u * P : (u + 1) * P], ident[:])
-            h_cols = keep.tile([P, 4 * C], BF16, name="h_cols%d" % e, tag="h_cols%d" % e, align_bytes=64)
+        def turn_and_quantize(experts, into):
+            count = len(experts)
+            turned = into[:, 0 : count * 2 * C].rearrange("p (e u j) -> p e u j", u=2, j=C)
+            for place, e in enumerate(experts):
+                pairs = rows[e][:].rearrange("j u p d -> j (u p d)").bitcast(F32)
+                for u in range(2):
+                    nc.tensor.transpose(turned[:, place, u, :], pairs[:, u * P : (u + 1) * P], ident[:])
+            h_cols = keep.tile([P, count * 4 * C], BF16, name="h_cols%d" % experts[0], align_bytes=64)
             nc.scalar.copy(
-                out=h_cols[:].bitcast(F32).rearrange("p (j u) -> p j u", u=2),
-                in_=turned.rearrange("p u j -> p j u"),
+                out=h_cols[:].bitcast(F32).rearrange("p (e j u) -> p e j u", u=2, j=C),
+                in_=turned.rearrange("p e u j -> p e j u"),
             )
-            nc.vector.quantize_mx(out=h_codes[e][:].bitcast(FP8X4), scales=h_scales[e][:], in_=h_cols[:])
+            codes = keep.tile([P, count * C], U32, name="h_codes%d" % experts[0], align_bytes=64)
+            scales = keep.tile([P, count * C], U8, name="h_scales%d" % experts[0], align_bytes=64)
+            nc.vector.quantize_mx(out=codes[:].bitcast(FP8X4), scales=scales[:], in_=h_cols[:])
+            for place, e in enumerate(experts):
+                h_codes[e] = codes[:, place * C : (place + 1) * C]
+                h_scales[e] = scales[:, place * C : (place + 1) * C]
 
         def second_product(e, hf, dst):
             nc.tensor.matmul_mx(
                 out=dst,
                 lhsT=w2_sb[:, e, 2 * hf * P : 2 * (hf + 1) * P].bitcast(FP4X4),
                 lhsT_scale=w2_plane[:, e, hf * P : (hf + 1) * P],
-                rhs=h_codes[e][:].bitcast(FP8X4),
-                rhs_scale=h_scales[e][:],
+                rhs=h_codes[e].bitcast(FP8X4),
+                rhs_scale=h_scales[e],
                 start=True,
                 stop=True,
             )
 
-        def second_layer_first_four():
-            for hf in range(HALVES):
-                y_acc = bank[3 if hf == 0 else 0]
-                for e in range(4):
-                    second_product(e, hf, y_acc[:, e * C : (e + 1) * C])
-                nc.scalar.copy(out=y_win[hf][:, 0 : 4 * C], in_=y_acc[:])
-
-        def second_layer(e):
-            y_acc = bank[4 if e == 4 else 1]
-            for hf in range(HALVES):
-                second_product(e, hf, y_acc[:, hf * C : (hf + 1) * C])
-            for hf in range(HALVES):
-                nc.scalar.copy(out=y_win[hf][:, e * C : (e + 1) * C], in_=y_acc[:, hf * C : (hf + 1) * C])
+        def second_layer(hf, experts, y_acc):
+            for place, e in enumerate(experts):
+                second_product(e, hf, y_acc[:, place * C : (place + 1) * C])
+            nc.scalar.copy(out=y_win[hf][:, experts[0] * C : (experts[-1] + 1) * C], in_=y_acc[:, 0 : len(experts) * C])
 
         rows = {}
         gather_tokens(0)
@@ -205,12 +203,17 @@ def tile_moe_ecr_glu_sigmoid_kernel(
                 parts[e] = first_layer(e)
             if e > 0:
                 rows[e - 1] = gated_product(e - 1, *parts[e - 1])
-                turn_and_quantize(e - 1, rows[e - 1])
             if e == 2:
                 gather_tokens(2)
-        second_layer_first_four()
-        second_layer(4)
-        second_layer(5)
+                turn_and_quantize((0, 1), bank[2])
+            if e == 4:
+                turn_and_quantize((2, 3), bank[7])
+            if e > 4:
+                turn_and_quantize((e - 1,), bank[e + 1])
+        second_layer(0, (0, 1, 2, 3), bank[3])
+        second_layer(0, (4, 5), bank[0])
+        second_layer(1, (0, 1, 2, 3), bank[0])
+        second_layer(1, (4, 5), bank[4])
 
         prod = [[keep.tile([P, T], F32, name="prod%d_%d" % (hf, r)) for r in range(TOP)] for hf in range(HALVES)]
         blocks = T // P

@@ -53,8 +53,7 @@ def tile_moe_ecr_glu_sigmoid_kernel(
 
         x_win = keep.tile([P, PASSES, T], I32, name="x_win", align_bytes=64)
         xs_win = keep.tile([P, PASSES, T], U8, name="xs_win", align_bytes=64)
-        stage = keep.tile([P, STAGE_COLS], I32, name="stage", align_bytes=64)
-        w13_plane = [keep.tile([P, 2, len(g) * PASSES, H], U8, name="w13_plane%d" % g[0], align_bytes=64) for g in SCALE_GROUPS]
+        w13_plane = [keep.tile([P, E * PASSES, H], U8, name="w%d_plane" % m, align_bytes=64) for m in (1, 3)]
         w2_plane = keep.tile([P, E, N], U8, name="w2_plane", align_bytes=64)
         w1_sb = [keep.tile([P, PASSES, 2 * H], U8, name="w1_sb%d" % e, tag="w1_sb%d" % e, align_bytes=64) for e in range(E)]
         w3_sb = [keep.tile([P, PASSES, 2 * H], U8, name="w3_sb%d" % e, align_bytes=64) for e in range(E)]
@@ -64,7 +63,7 @@ def tile_moe_ecr_glu_sigmoid_kernel(
         ident = keep.tile([P, P], F32, name="ident")
 
         nc.vector.memset(xs_win[:].bitcast(I32), 0)
-        for g in range(len(SCALE_GROUPS)):
+        for g in range(2):
             nc.vector.memset(w13_plane[g][:].bitcast(I32), 0)
         nc.gpsimd.memset(w2_plane[:].bitcast(I32), 0)
         for hf in range(HALVES):
@@ -79,41 +78,22 @@ def tile_moe_ecr_glu_sigmoid_kernel(
             for w_sb, w_all in ((w1_sb, w1_all), (w3_sb, w3_all)):
                 nc.sync.dma_start(out=w_sb[e][:].bitcast(I32), in_=w_all[:, e * PASSES : (e + 1) * PASSES, :])
 
-        def move_scale_rows(g):
-            experts = SCALE_GROUPS[g]
-            cols = slice(experts[0] * PASSES * ROW_WORDS, (experts[-1] + 1) * PASSES * ROW_WORDS)
-            for r in range(4):
-                nc.sync.dma_start(
-                    out=w13_plane[g][r:P:32].rearrange("p m a c -> p m (a c)").bitcast(I32),
-                    in_=stage[4 + 8 * r : P : 32, :].rearrange("p (m c) -> p m c", m=2)[:, :, cols],
-                )
-
         nc.sync.dma_start(out=x_win[:], in_=x_words.rearrange("s p t r -> p s (t r)").bitcast(I32))
         load_scale_rows(nc, xs_win, x_scales.bitcast(I32).rearrange("s (q r) c -> r q s c", r=4))
         nc.sync.dma_start(offs_sb[:], offs)
-        for m, scales in enumerate((w1_scales, w3_scales)):
-            nc.sync.dma_start(
-                out=stage[4:P:8, m * W13_COLS : (m + 1) * W13_COLS].rearrange("q (a c) -> q a c", c=ROW_WORDS),
-                in_=scales.bitcast(I32).rearrange("e s q c -> q (e s) c"),
-            )
-
         load_words(0)
+        for m, scales in enumerate((w1_scales, w3_scales)):
+            load_scale_rows(nc, w13_plane[m], scales.bitcast(I32).rearrange("e s (q r) c -> r q (e s) c", r=4))
+        load_scale_rows(nc, w2_plane, w2_rows)
         nc.sync.dma_start(pos_sb[0][:], pos1)
         nc.sync.dma_start(pos_sb[1][:], pos2)
-        move_scale_rows(0)
-        load_words(1)
-        move_scale_rows(1)
-        load_words(2)
-        load_words(3)
-        move_scale_rows(2)
-        load_scale_rows(nc, w2_plane, w2_rows)
-        nc.sync.dma_start(pos_sb[2][:], pos3)
-        nc.sync.dma_start(pos_sb[3][:], pos4)
-        load_words(4)
-        load_words(5)
+        for e in range(1, E):
+            load_words(e)
         nc.sync.dma_start(out=w2_sb[:].bitcast(I32), in_=w2_words.bitcast(I32).rearrange("e s p c -> p (e s) c"))
         for r in range(TOP):
             nc.sync.dma_start(out=gate_sb[r][:], in_=gate[r, 0:P, :])
+        nc.sync.dma_start(pos_sb[2][:], pos3)
+        nc.sync.dma_start(pos_sb[3][:], pos4)
 
         width = GATHER_GROUP * C
         x_slot = {}
@@ -121,7 +101,7 @@ def tile_moe_ecr_glu_sigmoid_kernel(
 
         def gather_tokens(g):
             picks = offs_sb[:, g * width // 16 : (g + 1) * width // 16]
-            last = g == E // GATHER_GROUP - 1
+            last = False
             x_slot[g] = [keep.tile([P, width], U32, name="x_slot%d_%d" % (g, s), tag="x_slot%d_%d" % (g, s), align_bytes=64) for s in range(PASSES)]
             xs_slot[g] = [keep.tile([P, width], U8, name="xs_slot%d_%d" % (g, s), tag="sig%d" % s if last else "xs_slot%d_%d" % (g, s), align_bytes=64) for s in range(PASSES)]
             for s in range(PASSES):
@@ -145,7 +125,7 @@ def tile_moe_ecr_glu_sigmoid_kernel(
                         lhsT=x_slot[g][s][:, cols].bitcast(FP8X4),
                         lhsT_scale=xs_slot[g][s][:, cols],
                         rhs=w_sb[e][:, s, :].bitcast(FP4X4),
-                        rhs_scale=w13_plane[sg][:, m, (e - SCALE_GROUPS[sg][0]) * PASSES + s, :],
+                        rhs_scale=w13_plane[m][:, e * PASSES + s, :],
                         start=(s == 0),
                         stop=(s == PASSES - 1),
                     )
@@ -155,7 +135,7 @@ def tile_moe_ecr_glu_sigmoid_kernel(
             return sig, sums[1]
 
         def gated_product(e, sig, b_sum):
-            h_rows = keep.tile([C, 2, P, 2], BF16, name="h_rows%d" % e, tag="h_rows%d" % e, align_bytes=64)
+            h_rows = keep.tile([C, 2, P, 2], BF16, name="h_rows%d" % e, tag=("w1_sb5" if e == 4 else "h_rows%d" % e), align_bytes=64)
             nc.vector.tensor_tensor(out=h_rows[:], in0=sig[:], in1=b_sum, op=MULT)
             return h_rows
 
@@ -171,7 +151,7 @@ def tile_moe_ecr_glu_sigmoid_kernel(
                 out=h_cols[:].bitcast(F32).rearrange("p (e j u) -> p e j u", u=2, j=C),
                 in_=turned.rearrange("p e u j -> p e j u"),
             )
-            codes = keep.tile([P, count * C], U32, name="h_codes%d" % experts[0], align_bytes=64)
+            codes = keep.tile([P, count * C], U32, name="h_codes%d" % experts[0], tag=("sig%d" % (experts[-1] + 1) if count == 2 else "h_codes%d" % experts[0]), align_bytes=64)
             scales = keep.tile([P, count * C], U8, name="h_scales%d" % experts[0], align_bytes=64)
             nc.vector.quantize_mx(out=codes[:].bitcast(FP8X4), scales=scales[:], in_=h_cols[:])
             for place, e in enumerate(experts):
@@ -197,17 +177,17 @@ def tile_moe_ecr_glu_sigmoid_kernel(
         rows = {}
         gather_tokens(0)
         gather_tokens(1)
+        gather_tokens(2)
         parts = {}
         for e in range(E + 1):
             if e < E:
                 parts[e] = first_layer(e)
             if e > 0:
                 rows[e - 1] = gated_product(e - 1, *parts[e - 1])
-            if e == 2:
-                gather_tokens(2)
+            if e == 3:
                 turn_and_quantize((0, 1), bank[2])
-            if e == 4:
-                turn_and_quantize((2, 3), bank[7])
+            if e == 5:
+                turn_and_quantize((2, 3), bank[1])
             if e > 4:
                 turn_and_quantize((e - 1,), bank[e + 1])
         second_layer(0, (0, 1, 2, 3), bank[3])

@@ -32,9 +32,9 @@ W13_COLS = E * PASSES * ROW_WORDS
 STAGE_COLS = 2 * W13_COLS
 
 
-def load_scale_rows(nc, plane, rows):
+def load_scale_rows(queue, plane, rows):
     for r in range(4):
-        nc.sync.dma_start(out=plane[r:P:32, :, :].bitcast(I32), in_=rows[r])
+        queue.dma_start(out=plane[r:P:32, :, :].bitcast(I32), in_=rows[r])
 
 
 def tile_moe_ecr_glu_sigmoid_kernel(
@@ -62,13 +62,18 @@ def tile_moe_ecr_glu_sigmoid_kernel(
         y_win = [keep.tile([P, SLOTS + PAD], F32, name="y_win%d" % hf) for hf in range(HALVES)]
         ident = keep.tile([P, P], F32, name="ident")
 
-        nc.vector.memset(xs_win[:].bitcast(I32), 0)
-        for g in range(2):
-            nc.vector.memset(w13_plane[g][:].bitcast(I32), 0)
-        nc.gpsimd.memset(w2_plane[:].bitcast(I32), 0)
-        for hf in range(HALVES):
-            nc.gpsimd.memset(y_win[hf][:, SLOTS:], 0.0)
         make_identity(nc, ident[:])
+        nc.vector.memset(w13_plane[0][:].bitcast(I32), 0)
+
+        def clear_one_port(words):
+            count = words.shape[1]
+            nc.vector.memset(words[:, 0 : count - 1], 0)
+            nc.vector.memset(words[:, count - 1 : count], 0)
+
+        for plane in (xs_win, w13_plane[1], w2_plane):
+            clear_one_port(plane[:].rearrange("p a c -> p (a c)").bitcast(I32))
+        for hf in range(HALVES):
+            nc.vector.memset(y_win[hf][:, SLOTS:], 0.0)
 
         w2_rows = w2_scales.bitcast(I32).rearrange("e s (q r) c -> r q (e s) c", r=4)
         w1_all = w1_words.bitcast(I32).rearrange("e s p c -> p (e s) c")
@@ -79,14 +84,14 @@ def tile_moe_ecr_glu_sigmoid_kernel(
                 nc.sync.dma_start(out=w_sb[e][:].bitcast(I32), in_=w_all[:, e * PASSES : (e + 1) * PASSES, :])
 
         nc.sync.dma_start(out=x_win[:], in_=x_words.rearrange("s p t r -> p s (t r)").bitcast(I32))
-        load_scale_rows(nc, xs_win, x_scales.bitcast(I32).rearrange("s (q r) c -> r q s c", r=4))
+        load_scale_rows(nc.sync, xs_win, x_scales.bitcast(I32).rearrange("s (q r) c -> r q s c", r=4))
         nc.sync.dma_start(offs_sb[:], offs)
         load_words(0)
-        for m, scales in enumerate((w1_scales, w3_scales)):
-            load_scale_rows(nc, w13_plane[m], scales.bitcast(I32).rearrange("e s (q r) c -> r q (e s) c", r=4))
-        load_scale_rows(nc, w2_plane, w2_rows)
         nc.sync.dma_start(pos_sb[0][:], pos1)
         nc.sync.dma_start(pos_sb[1][:], pos2)
+        for m, scales in enumerate((w1_scales, w3_scales)):
+            load_scale_rows((nc.gpsimd, nc.sync)[m], w13_plane[m], scales.bitcast(I32).rearrange("e s (q r) c -> r q (e s) c", r=4))
+        load_scale_rows(nc.sync, w2_plane, w2_rows)
         for e in range(1, E):
             load_words(e)
         nc.sync.dma_start(out=w2_sb[:].bitcast(I32), in_=w2_words.bitcast(I32).rearrange("e s p c -> p (e s) c"))

@@ -25,7 +25,7 @@ MULT = mybir.AluOpType.mult
 ADD = mybir.AluOpType.add
 SIGMOID = mybir.ActivationFunctionType.Sigmoid
 
-SCALE_GROUPS = ((0, 1), (2, 3), (4, 5))
+SCALE_GROUPS = ((0, 1), (2, 3, 4, 5))
 GATHER_GROUP = 2
 ROW_WORDS = H // 4
 W13_COLS = E * PASSES * ROW_WORDS
@@ -53,7 +53,7 @@ def tile_moe_ecr_glu_sigmoid_kernel(
 
         x_win = keep.tile([P, PASSES, T], I32, name="x_win", align_bytes=64)
         xs_win = keep.tile([P, PASSES, T], U8, name="xs_win", align_bytes=64)
-        w13_plane = [keep.tile([P, E * PASSES, H], U8, name="w%d_plane" % m, align_bytes=64) for m in (1, 3)]
+        w13_plane = [[keep.tile([P, len(g) * PASSES, H], U8, name="w%d_plane%d" % (m, g[0]), align_bytes=64) for g in SCALE_GROUPS] for m in (1, 3)]
         w2_plane = keep.tile([P, E, N], U8, name="w2_plane", align_bytes=64)
         w1_sb = [keep.tile([P, PASSES, 2 * H], U8, name="w1_sb%d" % e, tag="w1_sb%d" % e, align_bytes=64) for e in range(E)]
         w3_sb = [keep.tile([P, PASSES, 2 * H], U8, name="w3_sb%d" % e, align_bytes=64) for e in range(E)]
@@ -63,14 +63,14 @@ def tile_moe_ecr_glu_sigmoid_kernel(
         ident = keep.tile([P, P], F32, name="ident")
 
         make_identity(nc, ident[:])
-        nc.vector.memset(w13_plane[0][:].bitcast(I32), 0)
+        nc.vector.memset(w13_plane[0][1][:].bitcast(I32), 0)
 
         def clear_one_port(words):
             count = words.shape[1]
             nc.vector.memset(words[:, 0 : count - 1], 0)
             nc.vector.memset(words[:, count - 1 : count], 0)
 
-        for plane in (xs_win, w13_plane[1], w2_plane):
+        for plane in (xs_win, w13_plane[0][0], w13_plane[1][0], w13_plane[1][1], w2_plane):
             clear_one_port(plane[:].rearrange("p a c -> p (a c)").bitcast(I32))
         for hf in range(HALVES):
             nc.vector.memset(y_win[hf][:, SLOTS:], 0.0)
@@ -86,19 +86,27 @@ def tile_moe_ecr_glu_sigmoid_kernel(
         nc.sync.dma_start(out=x_win[:], in_=x_words.rearrange("s p t r -> p s (t r)").bitcast(I32))
         load_scale_rows(nc.sync, xs_win, x_scales.bitcast(I32).rearrange("s (q r) c -> r q s c", r=4))
         nc.sync.dma_start(offs_sb[:], offs)
+        w13_rows = [scales.bitcast(I32).rearrange("e s (q r) c -> r q (e s) c", r=4) for scales in (w1_scales, w3_scales)]
+
+        def load_group(queue, m, g):
+            experts = SCALE_GROUPS[g]
+            load_scale_rows(queue, w13_plane[m][g], w13_rows[m][:, :, experts[0] * PASSES : (experts[-1] + 1) * PASSES, :])
+
+        load_group(nc.gpsimd, 0, 1)
         load_words(0)
-        nc.sync.dma_start(pos_sb[0][:], pos1)
-        nc.sync.dma_start(pos_sb[1][:], pos2)
-        for m, scales in enumerate((w1_scales, w3_scales)):
-            load_scale_rows((nc.gpsimd, nc.sync)[m], w13_plane[m], scales.bitcast(I32).rearrange("e s (q r) c -> r q (e s) c", r=4))
+        load_group(nc.sync, 0, 0)
+        load_group(nc.sync, 1, 0)
+        load_words(1)
+        load_group(nc.sync, 1, 1)
+        load_words(2)
+        load_words(3)
         load_scale_rows(nc.sync, w2_plane, w2_rows)
-        for e in range(1, E):
-            load_words(e)
+        load_words(4)
+        load_words(5)
         nc.sync.dma_start(out=w2_sb[:].bitcast(I32), in_=w2_words.bitcast(I32).rearrange("e s p c -> p (e s) c"))
         for r in range(TOP):
+            nc.sync.dma_start(pos_sb[r][:], (pos1, pos2, pos3, pos4)[r])
             nc.sync.dma_start(out=gate_sb[r][:], in_=gate[r, 0:P, :])
-        nc.sync.dma_start(pos_sb[2][:], pos3)
-        nc.sync.dma_start(pos_sb[3][:], pos4)
 
         width = GATHER_GROUP * C
         x_slot = {}
@@ -120,7 +128,7 @@ def tile_moe_ecr_glu_sigmoid_kernel(
         def first_layer(e):
             g, place = divmod(e, GATHER_GROUP)
             cols = slice(place * C, (place + 1) * C)
-            sg = e // 2
+            sg = 0 if e in SCALE_GROUPS[0] else 1
             sums = []
             for m, w_sb in enumerate((w1_sb, w3_sb)):
                 acc = bank[3 * m + e % 3]
@@ -130,7 +138,7 @@ def tile_moe_ecr_glu_sigmoid_kernel(
                         lhsT=x_slot[g][s][:, cols].bitcast(FP8X4),
                         lhsT_scale=xs_slot[g][s][:, cols],
                         rhs=w_sb[e][:, s, :].bitcast(FP4X4),
-                        rhs_scale=w13_plane[m][:, e * PASSES + s, :],
+                        rhs_scale=w13_plane[m][sg][:, (e - SCALE_GROUPS[sg][0]) * PASSES + s, :],
                         start=(s == 0),
                         stop=(s == PASSES - 1),
                     )

@@ -63,6 +63,7 @@ def tile_moe_ecr_glu_sigmoid_kernel(
         ident = keep.tile([P, P], F32, name="ident")
 
         make_identity(nc, ident[:])
+        nc.vector.memset(xs_win[:].bitcast(I32), 0)
         nc.vector.memset(w13_plane[0][1][:].bitcast(I32), 0)
 
         def clear_one_port(words):
@@ -70,7 +71,7 @@ def tile_moe_ecr_glu_sigmoid_kernel(
             nc.vector.memset(words[:, 0 : count - 1], 0)
             nc.vector.memset(words[:, count - 1 : count], 0)
 
-        for plane in (xs_win, w13_plane[0][0], w13_plane[1][0], w13_plane[1][1], w2_plane):
+        for plane in (w13_plane[0][0], w13_plane[1][0], w13_plane[1][1], w2_plane):
             clear_one_port(plane[:].rearrange("p a c -> p (a c)").bitcast(I32))
         for hf in range(HALVES):
             nc.vector.memset(y_win[hf][:, SLOTS:], 0.0)
@@ -114,7 +115,7 @@ def tile_moe_ecr_glu_sigmoid_kernel(
 
         def gather_tokens(g):
             picks = offs_sb[:, g * width // 16 : (g + 1) * width // 16]
-            last = False
+            last = g == E // GATHER_GROUP - 1
             x_slot[g] = [keep.tile([P, width], U32, name="x_slot%d_%d" % (g, s), tag="x_slot%d_%d" % (g, s), align_bytes=64) for s in range(PASSES)]
             xs_slot[g] = [keep.tile([P, width], U8, name="xs_slot%d_%d" % (g, s), tag="sig%d" % s if last else "xs_slot%d_%d" % (g, s), align_bytes=64) for s in range(PASSES)]
             for s in range(PASSES):
@@ -190,13 +191,14 @@ def tile_moe_ecr_glu_sigmoid_kernel(
         rows = {}
         gather_tokens(0)
         gather_tokens(1)
-        gather_tokens(2)
         parts = {}
         for e in range(E + 1):
             if e < E:
                 parts[e] = first_layer(e)
             if e > 0:
                 rows[e - 1] = gated_product(e - 1, *parts[e - 1])
+            if e == 2:
+                gather_tokens(2)
             if e == 3:
                 turn_and_quantize((0, 1), bank[2])
             if e == 5:

@@ -101,9 +101,11 @@ def tile_moe_ecr_glu_sigmoid_kernel(
         load_group(nc.sync, 1, 1)
         load_words(2)
         load_words(3)
-        load_scale_rows(nc.sync, w2_plane, w2_rows)
         load_words(4)
-        load_words(5)
+        nc.sync.dma_start(out=w1_sb[5][:].bitcast(I32), in_=w1_all[:, 5 * PASSES : 6 * PASSES, :])
+        for s in range(PASSES):
+            nc.sync.dma_start(out=w3_sb[5][:, s, :].bitcast(I32), in_=w3_all[:, 5 * PASSES + s, :])
+        load_scale_rows(nc.sync, w2_plane, w2_rows)
         nc.sync.dma_start(out=w2_sb[:].bitcast(I32), in_=w2_words.bitcast(I32).rearrange("e s p c -> p (e s) c"))
         for r in range(TOP):
             nc.sync.dma_start(pos_sb[r][:], (pos1, pos2, pos3, pos4)[r])
@@ -150,7 +152,11 @@ def tile_moe_ecr_glu_sigmoid_kernel(
 
         def gated_product(e, sig, b_sum):
             h_rows = keep.tile([C, 2, P, 2], BF16, name="h_rows%d" % e, tag=("w1_sb5" if e == 4 else "h_rows%d" % e), align_bytes=64)
-            nc.vector.tensor_tensor(out=h_rows[:], in0=sig[:], in1=b_sum, op=MULT)
+            if e < E - 1:
+                nc.vector.tensor_tensor(out=h_rows[:], in0=sig[:], in1=b_sum, op=MULT)
+            else:
+                for u in range(2):
+                    nc.vector.tensor_tensor(out=h_rows[:, u], in0=sig[:, u], in1=b_sum[:, u], op=MULT)
             return h_rows
 
         def turn_and_quantize(experts, into):

@@ -27,6 +27,7 @@ SIGMOID = mybir.ActivationFunctionType.Sigmoid
 
 SCALE_GROUPS = ((0, 1), (2, 3, 4, 5))
 GATHER_GROUP = 2
+LIST_ORDER = (3, 2, 1, 0)
 ROW_WORDS = H // 4
 W13_COLS = E * PASSES * ROW_WORDS
 STAGE_COLS = 2 * W13_COLS
@@ -107,7 +108,7 @@ def tile_moe_ecr_glu_sigmoid_kernel(
             nc.sync.dma_start(out=w3_sb[5][:, s, :].bitcast(I32), in_=w3_all[:, 5 * PASSES + s, :])
         load_scale_rows(nc.sync, w2_plane, w2_rows)
         nc.sync.dma_start(out=w2_sb[:].bitcast(I32), in_=w2_words.bitcast(I32).rearrange("e s p c -> p (e s) c"))
-        for r in range(TOP):
+        for r in LIST_ORDER:
             nc.sync.dma_start(pos_sb[r][:], (pos1, pos2, pos3, pos4)[r])
             nc.sync.dma_start(out=gate_sb[r][:], in_=gate[r, 0:P, :])
 
@@ -167,7 +168,8 @@ def tile_moe_ecr_glu_sigmoid_kernel(
                 for u in range(2):
                     nc.tensor.transpose(turned[:, place, u, :], pairs[:, u * P : (u + 1) * P], ident[:])
             h_cols = keep.tile([P, count * 4 * C], BF16, name="h_cols%d" % experts[0], align_bytes=64)
-            nc.scalar.copy(
+            move = nc.vector.tensor_copy if experts == (4,) else nc.scalar.copy
+            move(
                 out=h_cols[:].bitcast(F32).rearrange("p (e j u) -> p e j u", u=2, j=C),
                 in_=turned.rearrange("p e u j -> p e j u"),
             )
@@ -192,7 +194,10 @@ def tile_moe_ecr_glu_sigmoid_kernel(
         def second_layer(hf, experts, y_acc):
             for place, e in enumerate(experts):
                 second_product(e, hf, y_acc[:, place * C : (place + 1) * C])
-            nc.scalar.copy(out=y_win[hf][:, experts[0] * C : (experts[-1] + 1) * C], in_=y_acc[:, 0 : len(experts) * C])
+
+        def keep_results(hf, experts, y_acc):
+            move = nc.vector.tensor_copy if experts == (2, 3) else nc.scalar.copy
+            move(out=y_win[hf][:, experts[0] * C : (experts[-1] + 1) * C], in_=y_acc[:, 0 : len(experts) * C])
 
         rows = {}
         gather_tokens(0)
@@ -207,45 +212,43 @@ def tile_moe_ecr_glu_sigmoid_kernel(
                 gather_tokens(2)
             if e == 3:
                 turn_and_quantize((0, 1), bank[2])
-            if e == 5:
-                turn_and_quantize((2, 3), bank[1])
-            if e > 4:
-                turn_and_quantize((e - 1,), bank[e + 1])
-        second_layer(0, (0, 1, 2, 3), bank[3])
-        second_layer(0, (4, 5), bank[0])
-        second_layer(1, (0, 1, 2, 3), bank[0])
-        second_layer(1, (4, 5), bank[4])
+        turn_and_quantize((2, 3), bank[2])
+        turn_and_quantize((4,), bank[6])
+        turn_and_quantize((5,), bank[7])
+        shares = ((0, (0, 1), 3), (0, (2, 3), 4), (0, (4, 5), 1), (1, (0, 1, 2, 3), 0), (1, (4, 5), 5))
+        for hf, experts, b in shares:
+            second_layer(hf, experts, bank[b])
+        for hf, experts, b in shares:
+            keep_results(hf, experts, bank[b])
 
         prod = [[keep.tile([P, T], F32, name="prod%d_%d" % (hf, r)) for r in range(TOP)] for hf in range(HALVES)]
-        blocks = T // P
 
         def fetch(hf, r):
             nc.vector.tensor_tensor(out=prod[hf][r][:], in0=y_win[hf][:].indirect(pos_sb[r][:]), in1=gate_sb[r][:], op=MULT)
 
-        back = []
+        pieces = ((0, 0, T, 2, 5), (1, 0, T // 2, 6, 3), (1, T // 2, T, 7, 0))
         for hf in range(HALVES):
-            sum_t = bank[2 + 4 * hf]
-            for r in range(TOP - 1):
+            mine = [piece for piece in pieces if piece[0] == hf]
+            for r in LIST_ORDER[:-1]:
                 fetch(hf, r)
-                for b in range(blocks):
-                    cols = slice(b * P, (b + 1) * P)
-                    nc.tensor.matmul(
-                        sum_t[:, cols],
-                        lhsT=prod[hf][r][:, cols],
-                        rhs=ident[:],
-                        is_transpose=True,
-                        start=(r == 0 and b == 0),
-                        stop=(r == TOP - 2 and b == blocks - 1),
-                    )
-            sum_sb = ring.tile([P, T], F32, name="sum_sb")
-            nc.scalar.copy(out=sum_sb[:], in_=sum_t[:])
-            back.append(bank[5 + 2 * hf])
-            for b in range(blocks):
-                cols = slice(b * P, (b + 1) * P)
-                nc.tensor.transpose(back[hf][:, cols], sum_sb[:, cols], ident[:])
+                for unused, first, last, sum_bank, back_bank in mine:
+                    for col in range(first, last, P):
+                        nc.tensor.matmul(
+                            bank[sum_bank][:, col - first : col - first + P],
+                            lhsT=prod[hf][r][:, col : col + P],
+                            rhs=ident[:],
+                            is_transpose=True,
+                            start=(r == LIST_ORDER[0] and col == first),
+                            stop=(r == LIST_ORDER[-2] and col == last - P),
+                        )
+            for unused, first, last, sum_bank, back_bank in mine:
+                sum_sb = keep.tile([P, last - first], F32, name="sum_sb%d" % sum_bank)
+                nc.scalar.copy(out=sum_sb[:], in_=bank[sum_bank][:, 0 : last - first])
+                for col in range(0, last - first, P):
+                    nc.tensor.transpose(bank[back_bank][:, col : col + P], sum_sb[:, col : col + P], ident[:])
         for hf in range(HALVES):
-            fetch(hf, TOP - 1)
-        for hf, cols in ((0, slice(0, T)), (1, slice(0, T // 2)), (1, slice(T // 2, T))):
-            result = keep.tile([P, cols.stop - cols.start], F32, name="result%d_%d" % (hf, cols.start))
-            nc.vector.tensor_tensor(out=result[:], in0=prod[hf][TOP - 1][:, cols], in1=back[hf][:, cols], op=ADD)
-            nc.sync.dma_start(out=out[hf * P : (hf + 1) * P, cols], in_=result[:])
+            fetch(hf, LIST_ORDER[-1])
+        for hf, first, last, sum_bank, back_bank in pieces:
+            result = keep.tile([P, last - first], F32, name="result%d" % sum_bank)
+            nc.vector.tensor_tensor(out=result[:], in0=prod[hf][LIST_ORDER[-1]][:, first:last], in1=bank[back_bank][:, 0 : last - first], op=ADD)
+            nc.sync.dma_start(out=out[hf * P : (hf + 1) * P, first:last], in_=result[:])

@@ -98,8 +98,8 @@ def tile_moe_ecr_glu_sigmoid_kernel(
         load_words(0)
         load_group(nc.sync, 0, 0)
         load_group(nc.sync, 1, 0)
-        load_words(1)
         load_group(nc.sync, 1, 1)
+        load_words(1)
         load_words(2)
         load_words(3)
         load_words(4)
@@ -223,8 +223,9 @@ def tile_moe_ecr_glu_sigmoid_kernel(
 
         prod = [[keep.tile([P, T], F32, name="prod%d_%d" % (hf, r)) for r in range(TOP)] for hf in range(HALVES)]
 
-        def fetch(hf, r):
-            nc.vector.tensor_tensor(out=prod[hf][r][:], in0=y_win[hf][:].indirect(pos_sb[r][:]), in1=gate_sb[r][:], op=MULT)
+        def fetch(hf, r, first=0, last=T):
+            picks = pos_sb[r][:, first // 16 : last // 16]
+            nc.vector.tensor_tensor(out=prod[hf][r][:, first:last], in0=y_win[hf][:].indirect(picks), in1=gate_sb[r][:, first:last], op=MULT)
 
         pieces = ((0, 0, T, 2, 5), (1, 0, T // 2, 6, 3), (1, T // 2, T, 7, 0))
         for hf in range(HALVES):
@@ -246,9 +247,14 @@ def tile_moe_ecr_glu_sigmoid_kernel(
                 nc.scalar.copy(out=sum_sb[:], in_=bank[sum_bank][:, 0 : last - first])
                 for col in range(0, last - first, P):
                     nc.tensor.transpose(bank[back_bank][:, col : col + P], sum_sb[:, col : col + P], ident[:])
-        for hf in range(HALVES):
-            fetch(hf, LIST_ORDER[-1])
-        for hf, first, last, sum_bank, back_bank in pieces:
+
+        def finish(hf, first, last, sum_bank, back_bank):
             result = keep.tile([P, last - first], F32, name="result%d" % sum_bank)
             nc.vector.tensor_tensor(out=result[:], in0=prod[hf][LIST_ORDER[-1]][:, first:last], in1=bank[back_bank][:, 0 : last - first], op=ADD)
             nc.sync.dma_start(out=out[hf * P : (hf + 1) * P, first:last], in_=result[:])
+
+        for place, piece in enumerate(pieces):
+            fetch(piece[0], LIST_ORDER[-1], piece[1], piece[2])
+            if place > 0:
+                finish(*pieces[place - 1])
+        finish(*pieces[-1])

@@ -82,7 +82,8 @@ def tile_moe_ecr_glu_sigmoid_kernel(
         w3_all = w3_words.bitcast(I32).rearrange("e s p c -> p (e s) c")
 
         def load_words(e):
-            for w_sb, w_all in ((w1_sb, w1_all), (w3_sb, w3_all)):
+            both = ((w1_sb, w1_all), (w3_sb, w3_all))
+            for w_sb, w_all in reversed(both) if e == SCALE_GROUPS[1][0] else both:
                 nc.sync.dma_start(out=w_sb[e][:].bitcast(I32), in_=w_all[:, e * PASSES : (e + 1) * PASSES, :])
 
         nc.sync.dma_start(out=x_win[:], in_=x_words.rearrange("s p t r -> p s (t r)").bitcast(I32))

@@ -10,6 +10,7 @@ SLOTS = E * C
 P = 128
 PASSES = K // 512
 HALVES = N // P
+LAST = E - 1
 
 FLOPS = 2 * SLOTS * (2 * K * H + H * N)
 
@@ -25,12 +26,9 @@ MULT = mybir.AluOpType.mult
 ADD = mybir.AluOpType.add
 SIGMOID = mybir.ActivationFunctionType.Sigmoid
 
-SCALE_GROUPS = ((0, 1), (2, 3, 4, 5))
+EARLY = (2, 2)
 GATHER_GROUP = 2
 LIST_ORDER = (3, 2, 1, 0)
-ROW_WORDS = H // 4
-W13_COLS = E * PASSES * ROW_WORDS
-STAGE_COLS = 2 * W13_COLS
 
 
 def load_scale_rows(queue, plane, rows):
@@ -45,7 +43,6 @@ def tile_moe_ecr_glu_sigmoid_kernel(
     with ExitStack() as ctx:
         lists = ctx.enter_context(tc.tile_pool(name="lists", bufs=1))
         keep = ctx.enter_context(tc.tile_pool(name="keep", bufs=1))
-        ring = ctx.enter_context(tc.tile_pool(name="ring", bufs=2))
         psum = ctx.enter_context(tc.psum_pool(name="psum", bufs=1))
         bank = [psum.tile([P, 512], F32, name="bank%d" % b) for b in range(8)]
 
@@ -54,64 +51,66 @@ def tile_moe_ecr_glu_sigmoid_kernel(
 
         x_win = keep.tile([P, PASSES, T], I32, name="x_win", align_bytes=64)
         xs_win = keep.tile([P, PASSES, T], U8, name="xs_win", align_bytes=64)
-        w13_plane = [[keep.tile([P, len(g) * PASSES, H], U8, name="w%d_plane%d" % (m, g[0]), align_bytes=64) for g in SCALE_GROUPS] for m in (1, 3)]
+        early_plane = [keep.tile([P, EARLY[m] * PASSES, H], U8, name="early_plane%d" % m, align_bytes=64) for m in range(2)]
+        late_plane = [keep.tile([P, (E - EARLY[m]) * PASSES, H], U8, name="late_plane%d" % m, align_bytes=64) for m in range(2)]
         w2_plane = keep.tile([P, E, N], U8, name="w2_plane", align_bytes=64)
-        w1_sb = [keep.tile([P, PASSES, 2 * H], U8, name="w1_sb%d" % e, tag="w1_sb%d" % e, align_bytes=64) for e in range(E)]
-        w3_sb = [keep.tile([P, PASSES, 2 * H], U8, name="w3_sb%d" % e, align_bytes=64) for e in range(E)]
-        w2_sb = keep.tile([P, E, 2 * N], U8, name="w2_sb", align_bytes=64)
+        w_sb = [[keep.tile([P, PASSES, 2 * H], U8, name="w_sb%d_%d" % (m, e), tag="w_sb%d_%d" % (m, e), align_bytes=64) for e in range(E)] for m in range(2)]
+        w2_sb = [keep.tile([P, E, 2 * P], U8, name="w2_sb%d" % hf, align_bytes=64) for hf in range(HALVES)]
         gate_sb = [keep.tile([P, T], F32, name="gate_sb%d" % r) for r in range(TOP)]
         y_win = [keep.tile([P, SLOTS + PAD], F32, name="y_win%d" % hf) for hf in range(HALVES)]
         ident = keep.tile([P, P], F32, name="ident")
 
         make_identity(nc, ident[:])
         nc.vector.memset(xs_win[:].bitcast(I32), 0)
-        nc.vector.memset(w13_plane[0][1][:].bitcast(I32), 0)
+        nc.vector.memset(late_plane[0][:].bitcast(I32), 0)
 
-        def clear_one_port(words):
+        def clear_one_port(plane):
+            words = plane[:].rearrange("p a c -> p (a c)").bitcast(I32)
             count = words.shape[1]
             nc.vector.memset(words[:, 0 : count - 1], 0)
             nc.vector.memset(words[:, count - 1 : count], 0)
 
-        for plane in (w13_plane[0][0], w13_plane[1][0], w13_plane[1][1], w2_plane):
-            clear_one_port(plane[:].rearrange("p a c -> p (a c)").bitcast(I32))
+        for plane in (early_plane[0], early_plane[1], late_plane[1], w2_plane):
+            clear_one_port(plane)
         for hf in range(HALVES):
             nc.vector.memset(y_win[hf][:, SLOTS:], 0.0)
 
-        w2_rows = w2_scales.bitcast(I32).rearrange("e s (q r) c -> r q (e s) c", r=4)
-        w1_all = w1_words.bitcast(I32).rearrange("e s p c -> p (e s) c")
-        w3_all = w3_words.bitcast(I32).rearrange("e s p c -> p (e s) c")
+        w_all = [words.bitcast(I32).rearrange("e s p c -> p (e s) c") for words in (w1_words, w3_words)]
+        w_rows = [scales.bitcast(I32).rearrange("e s (q r) c -> r q (e s) c", r=4) for scales in (w1_scales, w3_scales)]
+        w2_all = w2_words.bitcast(I32).rearrange("e s p c -> p (e s) c")
 
-        def load_words(e):
-            both = ((w1_sb, w1_all), (w3_sb, w3_all))
-            for w_sb, w_all in reversed(both) if e == SCALE_GROUPS[1][0] else both:
-                nc.sync.dma_start(out=w_sb[e][:].bitcast(I32), in_=w_all[:, e * PASSES : (e + 1) * PASSES, :])
+        def load_words(m, e, first=0, last=PASSES):
+            nc.sync.dma_start(out=w_sb[m][e][:, first:last, :].bitcast(I32), in_=w_all[m][:, e * PASSES + first : e * PASSES + last, :])
+
+        def load_list(r):
+            nc.sync.dma_start(pos_sb[r][:], (pos1, pos2, pos3, pos4)[r])
+            nc.sync.dma_start(out=gate_sb[r][:], in_=gate[r, 0:P, :])
+
+        def load_w2(hf):
+            nc.sync.dma_start(out=w2_sb[hf][:].bitcast(I32), in_=w2_all[:, :, hf * P // 2 : (hf + 1) * P // 2])
 
         nc.sync.dma_start(out=x_win[:], in_=x_words.rearrange("s p t r -> p s (t r)").bitcast(I32))
         load_scale_rows(nc.sync, xs_win, x_scales.bitcast(I32).rearrange("s (q r) c -> r q s c", r=4))
         nc.sync.dma_start(offs_sb[:], offs)
-        w13_rows = [scales.bitcast(I32).rearrange("e s (q r) c -> r q (e s) c", r=4) for scales in (w1_scales, w3_scales)]
-
-        def load_group(queue, m, g):
-            experts = SCALE_GROUPS[g]
-            load_scale_rows(queue, w13_plane[m][g], w13_rows[m][:, :, experts[0] * PASSES : (experts[-1] + 1) * PASSES, :])
-
-        load_group(nc.gpsimd, 0, 1)
-        load_words(0)
-        load_group(nc.sync, 0, 0)
-        load_group(nc.sync, 1, 0)
-        load_group(nc.sync, 1, 1)
-        load_words(1)
-        load_words(2)
-        load_words(3)
-        load_words(4)
-        nc.sync.dma_start(out=w1_sb[5][:].bitcast(I32), in_=w1_all[:, 5 * PASSES : 6 * PASSES, :])
+        load_scale_rows(nc.gpsimd, late_plane[0], w_rows[0][:, :, EARLY[0] * PASSES :, :])
+        for m in range(2):
+            load_words(m, 0)
+        for m in range(2):
+            load_scale_rows(nc.sync, early_plane[m], w_rows[m][:, :, 0 : EARLY[m] * PASSES, :])
+        load_scale_rows(nc.sync, late_plane[1], w_rows[1][:, :, EARLY[1] * PASSES :, :])
+        for e in range(1, LAST):
+            for m in (1, 0) if e == EARLY[0] else (0, 1):
+                load_words(m, e)
+        load_words(0, LAST)
         for s in range(PASSES):
-            nc.sync.dma_start(out=w3_sb[5][:, s, :].bitcast(I32), in_=w3_all[:, 5 * PASSES + s, :])
-        load_scale_rows(nc.sync, w2_plane, w2_rows)
-        nc.sync.dma_start(out=w2_sb[:].bitcast(I32), in_=w2_words.bitcast(I32).rearrange("e s p c -> p (e s) c"))
-        for r in LIST_ORDER:
-            nc.sync.dma_start(pos_sb[r][:], (pos1, pos2, pos3, pos4)[r])
-            nc.sync.dma_start(out=gate_sb[r][:], in_=gate[r, 0:P, :])
+            load_words(1, LAST, s, s + 1)
+        load_scale_rows(nc.sync, w2_plane, w2_scales.bitcast(I32).rearrange("e s (q r) c -> r q (e s) c", r=4))
+        load_w2(0)
+        load_list(LIST_ORDER[0])
+        load_list(LIST_ORDER[1])
+        load_w2(1)
+        load_list(LIST_ORDER[2])
+        load_list(LIST_ORDER[3])
 
         width = GATHER_GROUP * C
         x_slot = {}
@@ -120,60 +119,61 @@ def tile_moe_ecr_glu_sigmoid_kernel(
         def gather_tokens(g):
             picks = offs_sb[:, g * width // 16 : (g + 1) * width // 16]
             last = g == E // GATHER_GROUP - 1
-            x_slot[g] = [keep.tile([P, width], U32, name="x_slot%d_%d" % (g, s), tag="x_slot%d_%d" % (g, s), align_bytes=64) for s in range(PASSES)]
+            x_slot[g] = [keep.tile([P, width], U32, name="x_slot%d_%d" % (g, s), align_bytes=64) for s in range(PASSES)]
             xs_slot[g] = [keep.tile([P, width], U8, name="xs_slot%d_%d" % (g, s), tag="sig%d" % s if last else "xs_slot%d_%d" % (g, s), align_bytes=64) for s in range(PASSES)]
             for s in range(PASSES):
                 nc.vector.tensor_copy(out=x_slot[g][s][:], in_=x_win[:, s, :].bitcast(U32).indirect(picks))
             for s in range(PASSES):
                 nc.vector.tensor_copy(out=xs_slot[g][s][:], in_=xs_win[:, s, :].indirect(picks))
 
-        h_codes = {}
-        h_scales = {}
-
-        def first_layer(e):
+        def first_product(m, e):
             g, place = divmod(e, GATHER_GROUP)
             cols = slice(place * C, (place + 1) * C)
-            sg = 0 if e in SCALE_GROUPS[0] else 1
-            sums = []
-            for m, w_sb in enumerate((w1_sb, w3_sb)):
-                acc = bank[3 * m + e % 3]
-                for s in range(PASSES):
-                    nc.tensor.matmul_mx(
-                        out=acc[:],
-                        lhsT=x_slot[g][s][:, cols].bitcast(FP8X4),
-                        lhsT_scale=xs_slot[g][s][:, cols],
-                        rhs=w_sb[e][:, s, :].bitcast(FP4X4),
-                        rhs_scale=w13_plane[m][sg][:, (e - SCALE_GROUPS[sg][0]) * PASSES + s, :],
-                        start=(s == 0),
-                        stop=(s == PASSES - 1),
-                    )
-                sums.append(acc[:].rearrange("j (p u d) -> j u p d", u=2, d=2))
+            acc = bank[3 * m + e % 3]
+            for s in range(PASSES):
+                plane = early_plane[m][:, e * PASSES + s, :] if e < EARLY[m] else late_plane[m][:, (e - EARLY[m]) * PASSES + s, :]
+                nc.tensor.matmul_mx(
+                    out=acc[:],
+                    lhsT=x_slot[g][s][:, cols].bitcast(FP8X4),
+                    lhsT_scale=xs_slot[g][s][:, cols],
+                    rhs=w_sb[m][e][:, s, :].bitcast(FP4X4),
+                    rhs_scale=plane,
+                    start=(s == 0),
+                    stop=(s == PASSES - 1),
+                )
+            return acc[:].rearrange("j (p u d) -> j u p d", u=2, d=2)
+
+        def by_halves(e):
+            return (slice(0, 1), slice(1, 2)) if e == LAST else (slice(0, 2),)
+
+        def first_layer(e):
+            a_sum = first_product(0, e)
+            b_sum = first_product(1, e)
             sig = keep.tile([C, 2, P, 2], F32, name="sig%d" % e, tag="sig%d" % e, align_bytes=64)
-            nc.scalar.activation(out=sig[:], in_=sums[0], func=SIGMOID)
-            return sig, sums[1]
+            for us in by_halves(e):
+                nc.scalar.activation(out=sig[:, us], in_=a_sum[:, us], func=SIGMOID)
+            return sig, b_sum
+
+        h_rows = {}
 
         def gated_product(e, sig, b_sum):
-            h_rows = keep.tile([C, 2, P, 2], BF16, name="h_rows%d" % e, tag=("w1_sb5" if e == 4 else "h_rows%d" % e), align_bytes=64)
-            if e < E - 1:
-                nc.vector.tensor_tensor(out=h_rows[:], in0=sig[:], in1=b_sum, op=MULT)
-            else:
-                for u in range(2):
-                    nc.vector.tensor_tensor(out=h_rows[:, u], in0=sig[:, u], in1=b_sum[:, u], op=MULT)
-            return h_rows
+            h_rows[e] = keep.tile([C, 2, P, 2], BF16, name="h_rows%d" % e, tag=("w_sb0_5" if e == LAST - 1 else "h_rows%d" % e), align_bytes=64)
+            for us in by_halves(e):
+                nc.vector.tensor_tensor(out=h_rows[e][:, us], in0=sig[:, us], in1=b_sum[:, us], op=MULT)
+
+        h_codes = {}
+        h_scales = {}
 
         def turn_and_quantize(experts, into):
             count = len(experts)
             turned = into[:, 0 : count * 2 * C].rearrange("p (e u j) -> p e u j", u=2, j=C)
             for place, e in enumerate(experts):
-                pairs = rows[e][:].rearrange("j u p d -> j (u p d)").bitcast(F32)
+                pairs = h_rows[e][:].rearrange("j u p d -> j (u p d)").bitcast(F32)
                 for u in range(2):
                     nc.tensor.transpose(turned[:, place, u, :], pairs[:, u * P : (u + 1) * P], ident[:])
             h_cols = keep.tile([P, count * 4 * C], BF16, name="h_cols%d" % experts[0], align_bytes=64)
-            move = nc.vector.tensor_copy if experts == (4,) else nc.scalar.copy
-            move(
-                out=h_cols[:].bitcast(F32).rearrange("p (e j u) -> p e j u", u=2, j=C),
-                in_=turned.rearrange("p e u j -> p e j u"),
-            )
+            move = nc.vector.tensor_copy if experts == (LAST - 1,) else nc.scalar.copy
+            move(out=h_cols[:].bitcast(F32).rearrange("p (e j u) -> p e j u", u=2, j=C), in_=turned.rearrange("p e u j -> p e j u"))
             codes = keep.tile([P, count * C], U32, name="h_codes%d" % experts[0], tag=("sig%d" % (experts[-1] + 1) if count == 2 else "h_codes%d" % experts[0]), align_bytes=64)
             scales = keep.tile([P, count * C], U8, name="h_scales%d" % experts[0], align_bytes=64)
             nc.vector.quantize_mx(out=codes[:].bitcast(FP8X4), scales=scales[:], in_=h_cols[:])
@@ -181,26 +181,21 @@ def tile_moe_ecr_glu_sigmoid_kernel(
                 h_codes[e] = codes[:, place * C : (place + 1) * C]
                 h_scales[e] = scales[:, place * C : (place + 1) * C]
 
-        def second_product(e, hf, dst):
-            nc.tensor.matmul_mx(
-                out=dst,
-                lhsT=w2_sb[:, e, 2 * hf * P : 2 * (hf + 1) * P].bitcast(FP4X4),
-                lhsT_scale=w2_plane[:, e, hf * P : (hf + 1) * P],
-                rhs=h_codes[e].bitcast(FP8X4),
-                rhs_scale=h_scales[e],
-                start=True,
-                stop=True,
-            )
-
         def second_layer(hf, experts, y_acc):
             for place, e in enumerate(experts):
-                second_product(e, hf, y_acc[:, place * C : (place + 1) * C])
+                nc.tensor.matmul_mx(
+                    out=y_acc[:, place * C : (place + 1) * C],
+                    lhsT=w2_sb[hf][:, e, :].bitcast(FP4X4),
+                    lhsT_scale=w2_plane[:, e, hf * P : (hf + 1) * P],
+                    rhs=h_codes[e].bitcast(FP8X4),
+                    rhs_scale=h_scales[e],
+                    start=True,
+                    stop=True,
+                )
 
-        def keep_results(hf, experts, y_acc):
-            move = nc.vector.tensor_copy if experts == (2, 3) else nc.scalar.copy
+        def keep_results(hf, experts, y_acc, move):
             move(out=y_win[hf][:, experts[0] * C : (experts[-1] + 1) * C], in_=y_acc[:, 0 : len(experts) * C])
 
-        rows = {}
         gather_tokens(0)
         gather_tokens(1)
         parts = {}
@@ -208,7 +203,7 @@ def tile_moe_ecr_glu_sigmoid_kernel(
             if e < E:
                 parts[e] = first_layer(e)
             if e > 0:
-                rows[e - 1] = gated_product(e - 1, *parts[e - 1])
+                gated_product(e - 1, *parts[e - 1])
             if e == 2:
                 gather_tokens(2)
             if e == 3:
@@ -216,11 +211,17 @@ def tile_moe_ecr_glu_sigmoid_kernel(
         turn_and_quantize((2, 3), bank[2])
         turn_and_quantize((4,), bank[6])
         turn_and_quantize((5,), bank[7])
-        shares = ((0, (0, 1), 3), (0, (2, 3), 4), (0, (4, 5), 1), (1, (0, 1, 2, 3), 0), (1, (4, 5), 5))
-        for hf, experts, b in shares:
+        shares = (
+            (0, (0, 1), 3, nc.scalar.copy),
+            (0, (2, 3), 4, nc.scalar.copy),
+            (0, (4,), 1, nc.vector.tensor_copy),
+            (0, (5,), 0, nc.scalar.copy),
+            (1, (0, 1, 2, 3), 5, nc.scalar.copy),
+            (1, (4, 5), 6, nc.scalar.copy),
+        )
+        for hf, experts, b, move in shares:
             second_layer(hf, experts, bank[b])
-        for hf, experts, b in shares:
-            keep_results(hf, experts, bank[b])
+            keep_results(hf, experts, bank[b], move)
 
         prod = [[keep.tile([P, T], F32, name="prod%d_%d" % (hf, r)) for r in range(TOP)] for hf in range(HALVES)]
 
@@ -228,9 +229,9 @@ def tile_moe_ecr_glu_sigmoid_kernel(
             picks = pos_sb[r][:, first // 16 : last // 16]
             nc.vector.tensor_tensor(out=prod[hf][r][:, first:last], in0=y_win[hf][:].indirect(picks), in1=gate_sb[r][:, first:last], op=MULT)
 
-        pieces = ((0, 0, T, 2, 5), (1, 0, T // 2, 6, 3), (1, T // 2, T, 7, 0))
+        sums = ((0, 0, T, 6, 7), (1, 0, T // 2, 3, 1), (1, T // 2, T, 4, 0))
         for hf in range(HALVES):
-            mine = [piece for piece in pieces if piece[0] == hf]
+            mine = [part for part in sums if part[0] == hf]
             for r in LIST_ORDER[:-1]:
                 fetch(hf, r)
                 for unused, first, last, sum_bank, back_bank in mine:
@@ -249,9 +250,13 @@ def tile_moe_ecr_glu_sigmoid_kernel(
                 for col in range(0, last - first, P):
                     nc.tensor.transpose(bank[back_bank][:, col : col + P], sum_sb[:, col : col + P], ident[:])
 
-        def finish(hf, first, last, sum_bank, back_bank):
-            result = keep.tile([P, last - first], F32, name="result%d" % sum_bank)
-            nc.vector.tensor_tensor(out=result[:], in0=prod[hf][LIST_ORDER[-1]][:, first:last], in1=bank[back_bank][:, 0 : last - first], op=ADD)
+        pieces = ((0, 0, T, 7, 0), (1, 0, T // 2, 1, 0), (1, T // 2, 3 * T // 4, 0, T // 2), (1, 3 * T // 4, T, 0, T // 2))
+
+        def finish(hf, first, last, back_bank, bank_first):
+            result = keep.tile([P, last - first], F32, name="result%d_%d" % (hf, first))
+            nc.vector.tensor_tensor(
+                out=result[:], in0=prod[hf][LIST_ORDER[-1]][:, first:last], in1=bank[back_bank][:, first - bank_first : last - bank_first], op=ADD
+            )
             nc.sync.dma_start(out=out[hf * P : (hf + 1) * P, first:last], in_=result[:])
 
         for place, piece in enumerate(pieces):

@@ -27,6 +27,7 @@ ADD = mybir.AluOpType.add
 SIGMOID = mybir.ActivationFunctionType.Sigmoid
 
 EARLY = (2, 2)
+ALIGN = 256
 GATHER_GROUP = 2
 LIST_ORDER = (3, 2, 1, 0)
 
@@ -49,16 +50,16 @@ def tile_moe_ecr_glu_sigmoid_kernel(
         offs_sb = lists.tile([P, SLOTS // 16], U16, name="offs_sb")
         pos_sb = [lists.tile([P, T // 16], U16, name="pos_sb%d" % r) for r in range(TOP)]
 
-        x_win = keep.tile([P, PASSES, T], I32, name="x_win", align_bytes=64)
-        xs_win = keep.tile([P, PASSES, T], U8, name="xs_win", align_bytes=64)
-        early_plane = [keep.tile([P, EARLY[m] * PASSES, H], U8, name="early_plane%d" % m, align_bytes=64) for m in range(2)]
-        late_plane = [keep.tile([P, (E - EARLY[m]) * PASSES, H], U8, name="late_plane%d" % m, align_bytes=64) for m in range(2)]
-        w2_plane = keep.tile([P, E, N], U8, name="w2_plane", align_bytes=64)
-        w_sb = [[keep.tile([P, PASSES, 2 * H], U8, name="w_sb%d_%d" % (m, e), tag="w_sb%d_%d" % (m, e), align_bytes=64) for e in range(E)] for m in range(2)]
-        w2_sb = [keep.tile([P, E, 2 * P], U8, name="w2_sb%d" % hf, align_bytes=64) for hf in range(HALVES)]
-        gate_sb = [keep.tile([P, T], F32, name="gate_sb%d" % r) for r in range(TOP)]
-        y_win = [keep.tile([P, SLOTS + PAD], F32, name="y_win%d" % hf) for hf in range(HALVES)]
-        ident = keep.tile([P, P], F32, name="ident")
+        x_win = keep.tile([P, PASSES, T], I32, name="x_win", align_bytes=ALIGN)
+        xs_win = keep.tile([P, PASSES, T], U8, name="xs_win", align_bytes=ALIGN)
+        early_plane = [keep.tile([P, EARLY[m] * PASSES, H], U8, name="early_plane%d" % m, align_bytes=ALIGN) for m in range(2)]
+        late_plane = [keep.tile([P, (E - EARLY[m]) * PASSES, H], U8, name="late_plane%d" % m, align_bytes=ALIGN) for m in range(2)]
+        w2_plane = keep.tile([P, E, N], U8, name="w2_plane", align_bytes=ALIGN)
+        w_sb = [[keep.tile([P, PASSES, 2 * H], U8, name="w_sb%d_%d" % (m, e), tag="w_sb%d_%d" % (m, e), align_bytes=ALIGN) for e in range(E)] for m in range(2)]
+        w2_sb = keep.tile([P, E, 2 * N], U8, name="w2_sb", align_bytes=ALIGN)
+        gate_sb = [keep.tile([P, T], F32, name="gate_sb%d" % r, align_bytes=ALIGN) for r in range(TOP)]
+        y_win = [keep.tile([P, SLOTS + PAD], F32, name="y_win%d" % hf, align_bytes=ALIGN) for hf in range(HALVES)]
+        ident = keep.tile([P, P], F32, name="ident", align_bytes=ALIGN)
 
         make_identity(nc, ident[:])
         nc.vector.memset(xs_win[:].bitcast(I32), 0)
@@ -86,9 +87,6 @@ def tile_moe_ecr_glu_sigmoid_kernel(
             nc.sync.dma_start(pos_sb[r][:], (pos1, pos2, pos3, pos4)[r])
             nc.sync.dma_start(out=gate_sb[r][:], in_=gate[r, 0:P, :])
 
-        def load_w2(hf):
-            nc.sync.dma_start(out=w2_sb[hf][:].bitcast(I32), in_=w2_all[:, :, hf * P // 2 : (hf + 1) * P // 2])
-
         nc.sync.dma_start(out=x_win[:], in_=x_words.rearrange("s p t r -> p s (t r)").bitcast(I32))
         load_scale_rows(nc.sync, xs_win, x_scales.bitcast(I32).rearrange("s (q r) c -> r q s c", r=4))
         nc.sync.dma_start(offs_sb[:], offs)
@@ -98,19 +96,13 @@ def tile_moe_ecr_glu_sigmoid_kernel(
         for m in range(2):
             load_scale_rows(nc.sync, early_plane[m], w_rows[m][:, :, 0 : EARLY[m] * PASSES, :])
         load_scale_rows(nc.sync, late_plane[1], w_rows[1][:, :, EARLY[1] * PASSES :, :])
-        for e in range(1, LAST):
+        for e in range(1, E):
             for m in (1, 0) if e == EARLY[0] else (0, 1):
                 load_words(m, e)
-        load_words(0, LAST)
-        for s in range(PASSES):
-            load_words(1, LAST, s, s + 1)
         load_scale_rows(nc.sync, w2_plane, w2_scales.bitcast(I32).rearrange("e s (q r) c -> r q (e s) c", r=4))
-        load_w2(0)
-        load_list(LIST_ORDER[0])
-        load_list(LIST_ORDER[1])
-        load_w2(1)
-        load_list(LIST_ORDER[2])
-        load_list(LIST_ORDER[3])
+        nc.sync.dma_start(out=w2_sb[:].bitcast(I32), in_=w2_all)
+        for r in LIST_ORDER:
+            load_list(r)
 
         width = GATHER_GROUP * C
         x_slot = {}
@@ -119,8 +111,8 @@ def tile_moe_ecr_glu_sigmoid_kernel(
         def gather_tokens(g):
             picks = offs_sb[:, g * width // 16 : (g + 1) * width // 16]
             last = g == E // GATHER_GROUP - 1
-            x_slot[g] = [keep.tile([P, width], U32, name="x_slot%d_%d" % (g, s), align_bytes=64) for s in range(PASSES)]
-            xs_slot[g] = [keep.tile([P, width], U8, name="xs_slot%d_%d" % (g, s), tag="sig%d" % s if last else "xs_slot%d_%d" % (g, s), align_bytes=64) for s in range(PASSES)]
+            x_slot[g] = [keep.tile([P, width], U32, name="x_slot%d_%d" % (g, s), align_bytes=ALIGN) for s in range(PASSES)]
+            xs_slot[g] = [keep.tile([P, width], U8, name="xs_slot%d_%d" % (g, s), tag="sig%d" % s if last else "xs_slot%d_%d" % (g, s), align_bytes=ALIGN) for s in range(PASSES)]
             for s in range(PASSES):
                 nc.vector.tensor_copy(out=x_slot[g][s][:], in_=x_win[:, s, :].bitcast(U32).indirect(picks))
             for s in range(PASSES):
@@ -149,7 +141,7 @@ def tile_moe_ecr_glu_sigmoid_kernel(
         def first_layer(e):
             a_sum = first_product(0, e)
             b_sum = first_product(1, e)
-            sig = keep.tile([C, 2, P, 2], F32, name="sig%d" % e, tag="sig%d" % e, align_bytes=64)
+            sig = keep.tile([C, 2, P, 2], F32, name="sig%d" % e, tag="sig%d" % e, align_bytes=ALIGN)
             for us in by_halves(e):
                 nc.scalar.activation(out=sig[:, us], in_=a_sum[:, us], func=SIGMOID)
             return sig, b_sum
@@ -157,7 +149,7 @@ def tile_moe_ecr_glu_sigmoid_kernel(
         h_rows = {}
 
         def gated_product(e, sig, b_sum):
-            h_rows[e] = keep.tile([C, 2, P, 2], BF16, name="h_rows%d" % e, tag=("w_sb0_5" if e == LAST - 1 else "h_rows%d" % e), align_bytes=64)
+            h_rows[e] = keep.tile([C, 2, P, 2], BF16, name="h_rows%d" % e, align_bytes=ALIGN)
             for us in by_halves(e):
                 nc.vector.tensor_tensor(out=h_rows[e][:, us], in0=sig[:, us], in1=b_sum[:, us], op=MULT)
 
@@ -171,11 +163,11 @@ def tile_moe_ecr_glu_sigmoid_kernel(
                 pairs = h_rows[e][:].rearrange("j u p d -> j (u p d)").bitcast(F32)
                 for u in range(2):
                     nc.tensor.transpose(turned[:, place, u, :], pairs[:, u * P : (u + 1) * P], ident[:])
-            h_cols = keep.tile([P, count * 4 * C], BF16, name="h_cols%d" % experts[0], align_bytes=64)
+            h_cols = keep.tile([P, count * 4 * C], BF16, name="h_cols%d" % experts[0], align_bytes=ALIGN)
             move = nc.vector.tensor_copy if experts == (LAST - 1,) else nc.scalar.copy
             move(out=h_cols[:].bitcast(F32).rearrange("p (e j u) -> p e j u", u=2, j=C), in_=turned.rearrange("p e u j -> p e j u"))
-            codes = keep.tile([P, count * C], U32, name="h_codes%d" % experts[0], tag=("sig%d" % (experts[-1] + 1) if count == 2 else "h_codes%d" % experts[0]), align_bytes=64)
-            scales = keep.tile([P, count * C], U8, name="h_scales%d" % experts[0], align_bytes=64)
+            codes = keep.tile([P, count * C], U32, name="h_codes%d" % experts[0], tag=("sig%d" % (experts[-1] + 1) if count == 2 else "h_codes%d" % experts[0]), align_bytes=ALIGN)
+            scales = keep.tile([P, count * C], U8, name="h_scales%d" % experts[0], align_bytes=ALIGN)
             nc.vector.quantize_mx(out=codes[:].bitcast(FP8X4), scales=scales[:], in_=h_cols[:])
             for place, e in enumerate(experts):
                 h_codes[e] = codes[:, place * C : (place + 1) * C]
@@ -185,7 +177,7 @@ def tile_moe_ecr_glu_sigmoid_kernel(
             for place, e in enumerate(experts):
                 nc.tensor.matmul_mx(
                     out=y_acc[:, place * C : (place + 1) * C],
-                    lhsT=w2_sb[hf][:, e, :].bitcast(FP4X4),
+                    lhsT=w2_sb[:, e, 2 * hf * P : 2 * (hf + 1) * P].bitcast(FP4X4),
                     lhsT_scale=w2_plane[:, e, hf * P : (hf + 1) * P],
                     rhs=h_codes[e].bitcast(FP8X4),
                     rhs_scale=h_scales[e],
@@ -208,13 +200,13 @@ def tile_moe_ecr_glu_sigmoid_kernel(
                 gather_tokens(2)
             if e == 3:
                 turn_and_quantize((0, 1), bank[2])
-        turn_and_quantize((2, 3), bank[2])
+        turn_and_quantize((2, 3), bank[4])
         turn_and_quantize((4,), bank[6])
         turn_and_quantize((5,), bank[7])
         shares = (
             (0, (0, 1), 3, nc.scalar.copy),
-            (0, (2, 3), 4, nc.scalar.copy),
-            (0, (4,), 1, nc.vector.tensor_copy),
+            (0, (2, 3), 2, nc.vector.tensor_copy),
+            (0, (4,), 1, nc.scalar.copy),
             (0, (5,), 0, nc.scalar.copy),
             (1, (0, 1, 2, 3), 5, nc.scalar.copy),
             (1, (4, 5), 6, nc.scalar.copy),
@@ -223,13 +215,13 @@ def tile_moe_ecr_glu_sigmoid_kernel(
             second_layer(hf, experts, bank[b])
             keep_results(hf, experts, bank[b], move)
 
-        prod = [[keep.tile([P, T], F32, name="prod%d_%d" % (hf, r)) for r in range(TOP)] for hf in range(HALVES)]
+        prod = [[keep.tile([P, T], F32, name="prod%d_%d" % (hf, r), align_bytes=ALIGN) for r in range(TOP)] for hf in range(HALVES)]
 
         def fetch(hf, r, first=0, last=T):
             picks = pos_sb[r][:, first // 16 : last // 16]
             nc.vector.tensor_tensor(out=prod[hf][r][:, first:last], in0=y_win[hf][:].indirect(picks), in1=gate_sb[r][:, first:last], op=MULT)
 
-        sums = ((0, 0, T, 6, 7), (1, 0, T // 2, 3, 1), (1, T // 2, T, 4, 0))
+        sums = ((0, 0, T, 2, 7), (1, 0, T // 2, 3, 1), (1, T // 2, T, 4, 0))
         for hf in range(HALVES):
             mine = [part for part in sums if part[0] == hf]
             for r in LIST_ORDER[:-1]:
@@ -245,7 +237,7 @@ def tile_moe_ecr_glu_sigmoid_kernel(
                             stop=(r == LIST_ORDER[-2] and col == last - P),
                         )
             for unused, first, last, sum_bank, back_bank in mine:
-                sum_sb = keep.tile([P, last - first], F32, name="sum_sb%d" % sum_bank)
+                sum_sb = keep.tile([P, last - first], F32, name="sum_sb%d" % sum_bank, align_bytes=ALIGN)
                 nc.scalar.copy(out=sum_sb[:], in_=bank[sum_bank][:, 0 : last - first])
                 for col in range(0, last - first, P):
                     nc.tensor.transpose(bank[back_bank][:, col : col + P], sum_sb[:, col : col + P], ident[:])
@@ -253,7 +245,7 @@ def tile_moe_ecr_glu_sigmoid_kernel(
         pieces = ((0, 0, T, 7, 0), (1, 0, T // 2, 1, 0), (1, T // 2, 3 * T // 4, 0, T // 2), (1, 3 * T // 4, T, 0, T // 2))
 
         def finish(hf, first, last, back_bank, bank_first):
-            result = keep.tile([P, last - first], F32, name="result%d_%d" % (hf, first))
+            result = keep.tile([P, last - first], F32, name="result%d_%d" % (hf, first), align_bytes=ALIGN)
             nc.vector.tensor_tensor(
                 out=result[:], in0=prod[hf][LIST_ORDER[-1]][:, first:last], in1=bank[back_bank][:, first - bank_first : last - bank_first], op=ADD
             )

@@ -62,8 +62,8 @@ def tile_moe_ecr_glu_sigmoid_kernel(
         ident = keep.tile([P, P], F32, name="ident", align_bytes=ALIGN)
 
         make_identity(nc, ident[:])
-        nc.vector.memset(xs_win[:].bitcast(I32), 0)
-        nc.vector.memset(late_plane[0][:].bitcast(I32), 0)
+        for plane in (xs_win, early_plane[0], early_plane[1], late_plane[0]):
+            nc.vector.memset(plane[:].bitcast(I32), 0)
 
         def clear_one_port(plane):
             words = plane[:].rearrange("p a c -> p (a c)").bitcast(I32)
@@ -71,7 +71,7 @@ def tile_moe_ecr_glu_sigmoid_kernel(
             nc.vector.memset(words[:, 0 : count - 1], 0)
             nc.vector.memset(words[:, count - 1 : count], 0)
 
-        for plane in (early_plane[0], early_plane[1], late_plane[1], w2_plane):
+        for plane in (late_plane[1], w2_plane):
             clear_one_port(plane)
         for hf in range(HALVES):
             nc.vector.memset(y_win[hf][:, SLOTS:], 0.0)

@@ -28,6 +28,7 @@ SIGMOID = mybir.ActivationFunctionType.Sigmoid
 
 EARLY = (2, 2)
 ALIGN = 256
+ROW_ALIGN = 2048
 GATHER_GROUP = 2
 LIST_ORDER = (3, 2, 1, 0)
 
@@ -50,14 +51,14 @@ def tile_moe_ecr_glu_sigmoid_kernel(
         offs_sb = lists.tile([P, SLOTS // 16], U16, name="offs_sb")
         pos_sb = [lists.tile([P, T // 16], U16, name="pos_sb%d" % r) for r in range(TOP)]
 
-        x_win = keep.tile([P, PASSES, T], I32, name="x_win", align_bytes=ALIGN)
-        xs_win = keep.tile([P, PASSES, T], U8, name="xs_win", align_bytes=ALIGN)
-        early_plane = [keep.tile([P, EARLY[m] * PASSES, H], U8, name="early_plane%d" % m, align_bytes=ALIGN) for m in range(2)]
-        late_plane = [keep.tile([P, (E - EARLY[m]) * PASSES, H], U8, name="late_plane%d" % m, align_bytes=ALIGN) for m in range(2)]
-        w2_plane = keep.tile([P, E, N], U8, name="w2_plane", align_bytes=ALIGN)
-        w_sb = [[keep.tile([P, PASSES, 2 * H], U8, name="w_sb%d_%d" % (m, e), tag="w_sb%d_%d" % (m, e), align_bytes=ALIGN) for e in range(E)] for m in range(2)]
-        w2_sb = keep.tile([P, E, 2 * N], U8, name="w2_sb", align_bytes=ALIGN)
-        gate_sb = [keep.tile([P, T], F32, name="gate_sb%d" % r, align_bytes=ALIGN) for r in range(TOP)]
+        x_win = keep.tile([P, PASSES, T], I32, name="x_win", align_bytes=ROW_ALIGN)
+        xs_win = keep.tile([P, PASSES, T], U8, name="xs_win", align_bytes=ROW_ALIGN)
+        early_plane = [keep.tile([P, EARLY[m] * PASSES, H], U8, name="early_plane%d" % m, align_bytes=ROW_ALIGN) for m in range(2)]
+        late_plane = [keep.tile([P, (E - EARLY[m]) * PASSES, H], U8, name="late_plane%d" % m, align_bytes=ROW_ALIGN) for m in range(2)]
+        w2_plane = keep.tile([P, E, N], U8, name="w2_plane", align_bytes=ROW_ALIGN)
+        w_sb = [[keep.tile([P, PASSES, 2 * H], U8, name="w_sb%d_%d" % (m, e), tag="w_sb%d_%d" % (m, e), align_bytes=ROW_ALIGN) for e in range(E)] for m in range(2)]
+        w2_sb = keep.tile([P, E, 2 * N], U8, name="w2_sb", align_bytes=ROW_ALIGN)
+        gate_sb = [keep.tile([P, T], F32, name="gate_sb%d" % r, align_bytes=ROW_ALIGN) for r in range(TOP)]
         y_win = [keep.tile([P, SLOTS + PAD], F32, name="y_win%d" % hf, align_bytes=ALIGN) for hf in range(HALVES)]
         ident = keep.tile([P, P], F32, name="ident", align_bytes=ALIGN)
 
@@ -245,7 +246,7 @@ def tile_moe_ecr_glu_sigmoid_kernel(
         pieces = ((0, 0, T, 7, 0), (1, 0, T // 2, 1, 0), (1, T // 2, 3 * T // 4, 0, T // 2), (1, 3 * T // 4, T, 0, T // 2))
 
         def finish(hf, first, last, back_bank, bank_first):
-            result = keep.tile([P, last - first], F32, name="result%d_%d" % (hf, first), align_bytes=ALIGN)
+            result = keep.tile([P, last - first], F32, name="result%d_%d" % (hf, first), align_bytes=ROW_ALIGN)
             nc.vector.tensor_tensor(
                 out=result[:], in0=prod[hf][LIST_ORDER[-1]][:, first:last], in1=bank[back_bank][:, first - bank_first : last - bank_first], op=ADD
             )

@@ -84,10 +84,6 @@ def tile_moe_ecr_glu_sigmoid_kernel(
         def load_words(m, e, first=0, last=PASSES):
             nc.sync.dma_start(out=w_sb[m][e][:, first:last, :].bitcast(I32), in_=w_all[m][:, e * PASSES + first : e * PASSES + last, :])
 
-        def load_list(r):
-            nc.sync.dma_start(pos_sb[r][:], (pos1, pos2, pos3, pos4)[r])
-            nc.sync.dma_start(out=gate_sb[r][:], in_=gate[r, 0:P, :])
-
         nc.sync.dma_start(out=x_win[:], in_=x_words.rearrange("s p t r -> p s (t r)").bitcast(I32))
         load_scale_rows(nc.sync, xs_win, x_scales.bitcast(I32).rearrange("s (q r) c -> r q s c", r=4))
         nc.sync.dma_start(offs_sb[:], offs)
@@ -101,9 +97,11 @@ def tile_moe_ecr_glu_sigmoid_kernel(
             for m in (1, 0) if e == EARLY[0] else (0, 1):
                 load_words(m, e)
         load_scale_rows(nc.sync, w2_plane, w2_scales.bitcast(I32).rearrange("e s (q r) c -> r q (e s) c", r=4))
+        for r in LIST_ORDER:
+            nc.sync.dma_start(pos_sb[r][:], (pos1, pos2, pos3, pos4)[r])
         nc.sync.dma_start(out=w2_sb[:].bitcast(I32), in_=w2_all)
         for r in LIST_ORDER:
-            load_list(r)
+            nc.sync.dma_start(out=gate_sb[r][:], in_=gate[r, 0:P, :])
 
         width = GATHER_GROUP * C
         x_slot = {}
@@ -165,7 +163,7 @@ def tile_moe_ecr_glu_sigmoid_kernel(
                 for u in range(2):
                     nc.tensor.transpose(turned[:, place, u, :], pairs[:, u * P : (u + 1) * P], ident[:])
             h_cols = keep.tile([P, count * 4 * C], BF16, name="h_cols%d" % experts[0], align_bytes=ALIGN)
-            move = nc.vector.tensor_copy if experts == (LAST - 1,) else nc.scalar.copy
+            move = nc.vector.tensor_copy if experts == (3,) else nc.scalar.copy
             move(out=h_cols[:].bitcast(F32).rearrange("p (e j u) -> p e j u", u=2, j=C), in_=turned.rearrange("p e u j -> p e j u"))
             codes = keep.tile([P, count * C], U32, name="h_codes%d" % experts[0], tag=("sig%d" % (experts[-1] + 1) if count == 2 else "h_codes%d" % experts[0]), align_bytes=ALIGN)
             scales = keep.tile([P, count * C], U8, name="h_scales%d" % experts[0], align_bytes=ALIGN)
@@ -201,13 +199,14 @@ def tile_moe_ecr_glu_sigmoid_kernel(
                 gather_tokens(2)
             if e == 3:
                 turn_and_quantize((0, 1), bank[2])
-        turn_and_quantize((2, 3), bank[4])
+        turn_and_quantize((2,), bank[4])
+        turn_and_quantize((3,), bank[2])
         turn_and_quantize((4,), bank[6])
         turn_and_quantize((5,), bank[7])
         shares = (
             (0, (0, 1), 3, nc.scalar.copy),
-            (0, (2, 3), 2, nc.vector.tensor_copy),
-            (0, (4,), 1, nc.scalar.copy),
+            (0, (2, 3), 4, nc.scalar.copy),
+            (0, (4,), 1, nc.vector.tensor_copy),
             (0, (5,), 0, nc.scalar.copy),
             (1, (0, 1, 2, 3), 5, nc.scalar.copy),
             (1, (4, 5), 6, nc.scalar.copy),
@@ -222,38 +221,45 @@ def tile_moe_ecr_glu_sigmoid_kernel(
             picks = pos_sb[r][:, first // 16 : last // 16]
             nc.vector.tensor_tensor(out=prod[hf][r][:, first:last], in0=y_win[hf][:].indirect(picks), in1=gate_sb[r][:, first:last], op=MULT)
 
-        sums = ((0, 0, T, 2, 7), (1, 0, T // 2, 3, 1), (1, T // 2, T, 4, 0))
-        for hf in range(HALVES):
-            mine = [part for part in sums if part[0] == hf]
-            for r in LIST_ORDER[:-1]:
-                fetch(hf, r)
-                for unused, first, last, sum_bank, back_bank in mine:
-                    for col in range(first, last, P):
-                        nc.tensor.matmul(
-                            bank[sum_bank][:, col - first : col - first + P],
-                            lhsT=prod[hf][r][:, col : col + P],
-                            rhs=ident[:],
-                            is_transpose=True,
-                            start=(r == LIST_ORDER[0] and col == first),
-                            stop=(r == LIST_ORDER[-2] and col == last - P),
-                        )
-            for unused, first, last, sum_bank, back_bank in mine:
-                sum_sb = keep.tile([P, last - first], F32, name="sum_sb%d" % sum_bank, align_bytes=ALIGN)
-                nc.scalar.copy(out=sum_sb[:], in_=bank[sum_bank][:, 0 : last - first])
-                for col in range(0, last - first, P):
-                    nc.tensor.transpose(bank[back_bank][:, col : col + P], sum_sb[:, col : col + P], ident[:])
+        def add_turned(into, hf, r, first, last, lists):
+            for col in range(first, last, P):
+                nc.tensor.matmul(
+                    into[:, col - first : col - first + P],
+                    lhsT=prod[hf][r][:, col : col + P],
+                    rhs=ident[:],
+                    is_transpose=True,
+                    start=(r == lists[0] and col == first),
+                    stop=(r == lists[-1] and col == last - P),
+                )
 
-        pieces = ((0, 0, T, 7, 0), (1, 0, T // 2, 1, 0), (1, T // 2, 3 * T // 4, 0, T // 2), (1, 3 * T // 4, T, 0, T // 2))
+        def turn_back(summed, width_, name):
+            sum_sb = keep.tile([P, width_], F32, name=name, align_bytes=ALIGN)
+            nc.scalar.copy(out=sum_sb[:], in_=summed[:, 0:width_])
+            for col in range(0, width_, P):
+                nc.tensor.transpose(summed[:, col : col + P], sum_sb[:, col : col + P], ident[:])
 
-        def finish(hf, first, last, back_bank, bank_first):
-            result = keep.tile([P, last - first], F32, name="result%d_%d" % (hf, first), align_bytes=ROW_ALIGN)
-            nc.vector.tensor_tensor(
-                out=result[:], in0=prod[hf][LIST_ORDER[-1]][:, first:last], in1=bank[back_bank][:, first - bank_first : last - bank_first], op=ADD
-            )
-            nc.sync.dma_start(out=out[hf * P : (hf + 1) * P, first:last], in_=result[:])
+        for r in LIST_ORDER:
+            fetch(0, r)
+            add_turned(bank[2], 0, r, 0, T, LIST_ORDER)
+        turn_back(bank[2], T, "sum_first")
+        first_half = keep.tile([P, T], F32, name="first_half", align_bytes=ROW_ALIGN)
+        nc.scalar.copy(out=first_half[:], in_=bank[2][:])
+        nc.sync.dma_start(out=out[0:P, :], in_=first_half[:])
 
-        for place, piece in enumerate(pieces):
-            fetch(piece[0], LIST_ORDER[-1], piece[1], piece[2])
-            if place > 0:
-                finish(*pieces[place - 1])
-        finish(*pieces[-1])
+        block_bank = (bank[3], bank[4], bank[0], bank[1])
+        summed_lists = LIST_ORDER[:-1]
+        for r in summed_lists:
+            step = T // 2 if r == summed_lists[-1] else T
+            for first in range(0, T, step):
+                fetch(1, r, first, first + step)
+                for col in range(first, first + step, P):
+                    add_turned(block_bank[col // P], 1, r, col, col + P, summed_lists)
+        for block in range(T // P):
+            turn_back(block_bank[block], P, "sum_block%d" % block)
+        for first in range(0, T, T // 2):
+            fetch(1, LIST_ORDER[-1], first, first + T // 2)
+        for block in range(T // P):
+            cols = slice(block * P, (block + 1) * P)
+            result = keep.tile([P, P], F32, name="result%d" % block, align_bytes=ROW_ALIGN)
+            nc.vector.tensor_tensor(out=result[:], in0=prod[1][LIST_ORDER[-1]][:, cols], in1=block_bank[block][:, 0:P], op=ADD)
+            nc.sync.dma_start(out=out[P : 2 * P, cols], in_=result[:])

@@ -238,18 +238,22 @@ def tile_moe_ecr_glu_sigmoid_kernel(
             for col in range(0, width_, P):
                 nc.tensor.transpose(summed[:, col : col + P], sum_sb[:, col : col + P], ident[:])
 
+        pair_bank = (bank[2], bank[7])
         for r in LIST_ORDER:
             fetch(0, r)
-            add_turned(bank[2], 0, r, 0, T, LIST_ORDER)
-        turn_back(bank[2], T, "sum_first")
+            for pair in range(2):
+                add_turned(pair_bank[pair], 0, r, pair * 2 * P, (pair + 1) * 2 * P, LIST_ORDER)
+        for pair in range(2):
+            turn_back(pair_bank[pair], 2 * P, "sum_pair%d" % pair)
         first_half = keep.tile([P, T], F32, name="first_half", align_bytes=ROW_ALIGN)
-        nc.scalar.copy(out=first_half[:], in_=bank[2][:])
+        for pair in range(2):
+            nc.scalar.copy(out=first_half[:, pair * 2 * P : (pair + 1) * 2 * P], in_=pair_bank[pair][:, 0 : 2 * P])
         nc.sync.dma_start(out=out[0:P, :], in_=first_half[:])
 
         block_bank = (bank[3], bank[4], bank[0], bank[1])
         summed_lists = LIST_ORDER[:-1]
         for r in summed_lists:
-            step = T // 2 if r == summed_lists[-1] else T
+            step = P if r == summed_lists[-1] else T
             for first in range(0, T, step):
                 fetch(1, r, first, first + step)
                 for col in range(first, first + step, P):

@@ -59,7 +59,7 @@ def tile_moe_ecr_glu_sigmoid_kernel(
         w_sb = [[keep.tile([P, PASSES, 2 * H], U8, name="w_sb%d_%d" % (m, e), tag="w_sb%d_%d" % (m, e), align_bytes=ROW_ALIGN) for e in range(E)] for m in range(2)]
         w2_sb = keep.tile([P, E, 2 * N], U8, name="w2_sb", align_bytes=ROW_ALIGN)
         gate_sb = [keep.tile([P, T], F32, name="gate_sb%d" % r, align_bytes=ROW_ALIGN) for r in range(TOP)]
-        y_win = [keep.tile([P, SLOTS + PAD], F32, name="y_win%d" % hf, align_bytes=ALIGN) for hf in range(HALVES)]
+        y_win = [keep.tile([P, SLOTS + PAD], F32, name="y_win0", align_bytes=ALIGN)]
         ident = keep.tile([P, P], F32, name="ident", align_bytes=ALIGN)
 
         make_identity(nc, ident[:])
@@ -74,8 +74,7 @@ def tile_moe_ecr_glu_sigmoid_kernel(
 
         for plane in (late_plane[1], w2_plane):
             clear_one_port(plane)
-        for hf in range(HALVES):
-            nc.vector.memset(y_win[hf][:, SLOTS:], 0.0)
+        nc.vector.memset(y_win[0][:, SLOTS:], 0.0)
 
         w_all = [words.bitcast(I32).rearrange("e s p c -> p (e s) c") for words in (w1_words, w3_words)]
         w_rows = [scales.bitcast(I32).rearrange("e s (q r) c -> r q (e s) c", r=4) for scales in (w1_scales, w3_scales)]
@@ -97,9 +96,9 @@ def tile_moe_ecr_glu_sigmoid_kernel(
             for m in (1, 0) if e == EARLY[0] else (0, 1):
                 load_words(m, e)
         load_scale_rows(nc.sync, w2_plane, w2_scales.bitcast(I32).rearrange("e s (q r) c -> r q (e s) c", r=4))
+        nc.sync.dma_start(out=w2_sb[:].bitcast(I32), in_=w2_all)
         for r in LIST_ORDER:
             nc.sync.dma_start(pos_sb[r][:], (pos1, pos2, pos3, pos4)[r])
-        nc.sync.dma_start(out=w2_sb[:].bitcast(I32), in_=w2_all)
         for r in LIST_ORDER:
             nc.sync.dma_start(out=gate_sb[r][:], in_=gate[r, 0:P, :])
 
@@ -155,19 +154,23 @@ def tile_moe_ecr_glu_sigmoid_kernel(
         h_codes = {}
         h_scales = {}
 
-        def turn_and_quantize(experts, into):
+        h_cols = {}
+
+        def turn(experts, into, move):
             count = len(experts)
             turned = into[:, 0 : count * 2 * C].rearrange("p (e u j) -> p e u j", u=2, j=C)
             for place, e in enumerate(experts):
                 pairs = h_rows[e][:].rearrange("j u p d -> j (u p d)").bitcast(F32)
                 for u in range(2):
                     nc.tensor.transpose(turned[:, place, u, :], pairs[:, u * P : (u + 1) * P], ident[:])
-            h_cols = keep.tile([P, count * 4 * C], BF16, name="h_cols%d" % experts[0], align_bytes=ALIGN)
-            move = nc.vector.tensor_copy if experts == (3,) else nc.scalar.copy
-            move(out=h_cols[:].bitcast(F32).rearrange("p (e j u) -> p e j u", u=2, j=C), in_=turned.rearrange("p e u j -> p e j u"))
-            codes = keep.tile([P, count * C], U32, name="h_codes%d" % experts[0], tag=("sig%d" % (experts[-1] + 1) if count == 2 else "h_codes%d" % experts[0]), align_bytes=ALIGN)
+            h_cols[experts] = keep.tile([P, count * 4 * C], BF16, name="h_cols%d" % experts[0], align_bytes=ALIGN)
+            move(out=h_cols[experts][:].bitcast(F32).rearrange("p (e j u) -> p e j u", u=2, j=C), in_=turned.rearrange("p e u j -> p e j u"))
+
+        def quantize(experts):
+            count = len(experts)
+            codes = keep.tile([P, count * C], U32, name="h_codes%d" % experts[0], tag=("sig2" if count == 2 else "h_codes%d" % experts[0]), align_bytes=ALIGN)
             scales = keep.tile([P, count * C], U8, name="h_scales%d" % experts[0], align_bytes=ALIGN)
-            nc.vector.quantize_mx(out=codes[:].bitcast(FP8X4), scales=scales[:], in_=h_cols[:])
+            nc.vector.quantize_mx(out=codes[:].bitcast(FP8X4), scales=scales[:], in_=h_cols[experts][:])
             for place, e in enumerate(experts):
                 h_codes[e] = codes[:, place * C : (place + 1) * C]
                 h_scales[e] = scales[:, place * C : (place + 1) * C]
@@ -198,11 +201,13 @@ def tile_moe_ecr_glu_sigmoid_kernel(
             if e == 2:
                 gather_tokens(2)
             if e == 3:
-                turn_and_quantize((0, 1), bank[2])
-        turn_and_quantize((2,), bank[4])
-        turn_and_quantize((3,), bank[2])
-        turn_and_quantize((4,), bank[6])
-        turn_and_quantize((5,), bank[7])
+                turn((0, 1), bank[2], nc.scalar.copy)
+                quantize((0, 1))
+        late_turns = ((2, 4, nc.scalar.copy), (4, 6, nc.vector.tensor_copy), (3, 2, nc.scalar.copy), (5, 7, nc.scalar.copy))
+        for e, b, move in late_turns:
+            turn((e,), bank[b], move)
+        for e, b, move in late_turns:
+            quantize((e,))
         shares = (
             (0, (0, 1), 3, nc.scalar.copy),
             (0, (2, 3), 4, nc.scalar.copy),
@@ -213,9 +218,10 @@ def tile_moe_ecr_glu_sigmoid_kernel(
         )
         for hf, experts, b, move in shares:
             second_layer(hf, experts, bank[b])
-            keep_results(hf, experts, bank[b], move)
+            if hf == 0:
+                keep_results(hf, experts, bank[b], move)
 
-        prod = [[keep.tile([P, T], F32, name="prod%d_%d" % (hf, r), align_bytes=ALIGN) for r in range(TOP)] for hf in range(HALVES)]
+        prod = [[keep.tile([P, T], F32, name="prod%d_%d" % (hf, r), tag="prod%d_%d" % (hf, r), align_bytes=ALIGN) for r in range(TOP)] for hf in range(HALVES)]
 
         def fetch(hf, r, first=0, last=T):
             picks = pos_sb[r][:, first // 16 : last // 16]
@@ -243,6 +249,12 @@ def tile_moe_ecr_glu_sigmoid_kernel(
             fetch(0, r)
             for pair in range(2):
                 add_turned(pair_bank[pair], 0, r, pair * 2 * P, (pair + 1) * 2 * P, LIST_ORDER)
+            if r == LIST_ORDER[0]:
+                y_win.append(keep.tile([P, SLOTS + PAD], F32, name="y_win1", tag="prod0_%d" % r, align_bytes=ALIGN))
+                nc.gpsimd.memset(y_win[1][:, SLOTS:], 0.0)
+                for hf, experts, b, move in shares:
+                    if hf == 1:
+                        keep_results(hf, experts, bank[b], move)
         for pair in range(2):
             turn_back(pair_bank[pair], 2 * P, "sum_pair%d" % pair)
         first_half = keep.tile([P, T], F32, name="first_half", align_bytes=ROW_ALIGN)

@@ -30,7 +30,9 @@ EARLY = (2, 2)
 ALIGN = 256
 ROW_ALIGN = 2048
 GATHER_GROUP = 2
-LIST_ORDER = (3, 2, 1, 0)
+COPY = mybir.ActivationFunctionType.Copy
+LIST_LOADS = (0, 3, 2, 1)
+GATE_LOADS = (3, 2, 0, 1)
 
 
 def load_scale_rows(queue, plane, rows):
@@ -58,8 +60,8 @@ def tile_moe_ecr_glu_sigmoid_kernel(
         w2_plane = keep.tile([P, E, N], U8, name="w2_plane", align_bytes=ROW_ALIGN)
         w_sb = [[keep.tile([P, PASSES, 2 * H], U8, name="w_sb%d_%d" % (m, e), tag="w_sb%d_%d" % (m, e), align_bytes=ROW_ALIGN) for e in range(E)] for m in range(2)]
         w2_sb = keep.tile([P, E, 2 * N], U8, name="w2_sb", align_bytes=ROW_ALIGN)
-        gate_sb = [keep.tile([P, T], F32, name="gate_sb%d" % r, align_bytes=ROW_ALIGN) for r in range(TOP)]
-        y_win = [keep.tile([P, SLOTS + PAD], F32, name="y_win0", align_bytes=ALIGN)]
+        gate_sb = [keep.tile([P, T], F32, name="gate_sb%d" % r, tag="gate_sb%d" % r, align_bytes=ROW_ALIGN) for r in range(TOP)]
+        y_win = [keep.tile([P, SLOTS + PAD], F32, name="y_win%d" % hf, align_bytes=ALIGN) for hf in range(HALVES)]
         ident = keep.tile([P, P], F32, name="ident", align_bytes=ALIGN)
 
         make_identity(nc, ident[:])
@@ -74,7 +76,8 @@ def tile_moe_ecr_glu_sigmoid_kernel(
 
         for plane in (late_plane[1], w2_plane):
             clear_one_port(plane)
-        nc.vector.memset(y_win[0][:, SLOTS:], 0.0)
+        for hf in range(HALVES):
+            nc.vector.memset(y_win[hf][:, SLOTS:], 0.0)
 
         w_all = [words.bitcast(I32).rearrange("e s p c -> p (e s) c") for words in (w1_words, w3_words)]
         w_rows = [scales.bitcast(I32).rearrange("e s (q r) c -> r q (e s) c", r=4) for scales in (w1_scales, w3_scales)]
@@ -97,9 +100,9 @@ def tile_moe_ecr_glu_sigmoid_kernel(
                 load_words(m, e)
         load_scale_rows(nc.sync, w2_plane, w2_scales.bitcast(I32).rearrange("e s (q r) c -> r q (e s) c", r=4))
         nc.sync.dma_start(out=w2_sb[:].bitcast(I32), in_=w2_all)
-        for r in LIST_ORDER:
+        for r in LIST_LOADS:
             nc.sync.dma_start(pos_sb[r][:], (pos1, pos2, pos3, pos4)[r])
-        for r in LIST_ORDER:
+        for r in GATE_LOADS:
             nc.sync.dma_start(out=gate_sb[r][:], in_=gate[r, 0:P, :])
 
         width = GATHER_GROUP * C
@@ -213,69 +216,78 @@ def tile_moe_ecr_glu_sigmoid_kernel(
             (0, (2, 3), 4, nc.scalar.copy),
             (0, (4,), 1, nc.vector.tensor_copy),
             (0, (5,), 0, nc.scalar.copy),
-            (1, (0, 1, 2, 3), 5, nc.scalar.copy),
+            (1, (0, 1, 2, 3), 7, nc.vector.tensor_copy),
             (1, (4, 5), 6, nc.scalar.copy),
         )
         for hf, experts, b, move in shares:
             second_layer(hf, experts, bank[b])
-            if hf == 0:
-                keep_results(hf, experts, bank[b], move)
+            keep_results(hf, experts, bank[b], move)
 
-        prod = [[keep.tile([P, T], F32, name="prod%d_%d" % (hf, r), tag="prod%d_%d" % (hf, r), align_bytes=ALIGN) for r in range(TOP)] for hf in range(HALVES)]
+        tiles = {}
 
-        def fetch(hf, r, first=0, last=T):
-            picks = pos_sb[r][:, first // 16 : last // 16]
-            nc.vector.tensor_tensor(out=prod[hf][r][:, first:last], in0=y_win[hf][:].indirect(picks), in1=gate_sb[r][:, first:last], op=MULT)
+        def row_tile(name, after=None):
+            tiles[name] = keep.tile([P, T], F32, name=name, tag=after or name, align_bytes=ROW_ALIGN)
+            return tiles[name]
 
-        def add_turned(into, hf, r, first, last, lists):
-            for col in range(first, last, P):
+        def fetch_times_gate(hf, r, after=None):
+            prod = row_tile("prod%d_%d" % (hf, r), after)
+            nc.vector.tensor_tensor(out=prod[:], in0=y_win[hf][:].indirect(pos_sb[r][:]), in1=gate_sb[r][:], op=MULT)
+
+        def fetch_raw(hf, r, after=None):
+            raw = row_tile("raw%d_%d" % (hf, r), after)
+            nc.scalar.activation(out=raw[:], in_=y_win[hf][:].indirect(pos_sb[r][:]), func=COPY)
+
+        def times_gate(hf, r, after=None):
+            prod = row_tile("prod%d_%d" % (hf, r), after)
+            nc.vector.tensor_tensor(out=prod[:], in0=tiles["raw%d_%d" % (hf, r)][:], in1=gate_sb[r][:], op=MULT)
+
+        def add_turned(banks, hf, r, lists):
+            share = T // len(banks)
+            for col in range(0, T, P):
                 nc.tensor.matmul(
-                    into[:, col - first : col - first + P],
-                    lhsT=prod[hf][r][:, col : col + P],
+                    banks[col // share][:, col % share : col % share + P],
+                    lhsT=tiles["prod%d_%d" % (hf, r)][:, col : col + P],
                     rhs=ident[:],
                     is_transpose=True,
-                    start=(r == lists[0] and col == first),
-                    stop=(r == lists[-1] and col == last - P),
+                    start=(r == lists[0] and col % share == 0),
+                    stop=(r == lists[-1] and col % share == share - P),
                 )
 
-        def turn_back(summed, width_, name):
-            sum_sb = keep.tile([P, width_], F32, name=name, align_bytes=ALIGN)
-            nc.scalar.copy(out=sum_sb[:], in_=summed[:, 0:width_])
-            for col in range(0, width_, P):
-                nc.tensor.transpose(summed[:, col : col + P], sum_sb[:, col : col + P], ident[:])
+        def turn_back(banks, hf):
+            share = T // len(banks)
+            summed = row_tile("sum%d" % hf)
+            for place, held in enumerate(banks):
+                nc.scalar.copy(out=summed[:, place * share : (place + 1) * share], in_=held[:, 0:share])
+                for col in range(0, share, P):
+                    nc.tensor.transpose(held[:, col : col + P], summed[:, place * share + col : place * share + col + P], ident[:])
 
-        pair_bank = (bank[2], bank[7])
-        for r in LIST_ORDER:
-            fetch(0, r)
-            for pair in range(2):
-                add_turned(pair_bank[pair], 0, r, pair * 2 * P, (pair + 1) * 2 * P, LIST_ORDER)
-            if r == LIST_ORDER[0]:
-                y_win.append(keep.tile([P, SLOTS + PAD], F32, name="y_win1", tag="prod0_%d" % r, align_bytes=ALIGN))
-                nc.gpsimd.memset(y_win[1][:, SLOTS:], 0.0)
-                for hf, experts, b, move in shares:
-                    if hf == 1:
-                        keep_results(hf, experts, bank[b], move)
-        for pair in range(2):
-            turn_back(pair_bank[pair], 2 * P, "sum_pair%d" % pair)
-        first_half = keep.tile([P, T], F32, name="first_half", align_bytes=ROW_ALIGN)
-        for pair in range(2):
-            nc.scalar.copy(out=first_half[:, pair * 2 * P : (pair + 1) * 2 * P], in_=pair_bank[pair][:, 0 : 2 * P])
-        nc.sync.dma_start(out=out[0:P, :], in_=first_half[:])
+        def finish(banks, hf, piece, after=None):
+            share = T // len(banks)
+            result = row_tile("result%d" % hf, after)
+            for col in range(0, T, piece):
+                cols = slice(col, col + piece)
+                nc.vector.tensor_tensor(out=result[:, cols], in0=tiles["prod%d_1" % hf][:, cols], in1=banks[col // share][:, col % share : col % share + piece], op=ADD)
+                nc.sync.dma_start(out=out[hf * P : (hf + 1) * P, cols], in_=result[:, cols])
 
-        block_bank = (bank[3], bank[4], bank[0], bank[1])
-        summed_lists = LIST_ORDER[:-1]
-        for r in summed_lists:
-            step = P if r == summed_lists[-1] else T
-            for first in range(0, T, step):
-                fetch(1, r, first, first + step)
-                for col in range(first, first + step, P):
-                    add_turned(block_bank[col // P], 1, r, col, col + P, summed_lists)
-        for block in range(T // P):
-            turn_back(block_bank[block], P, "sum_block%d" % block)
-        for first in range(0, T, T // 2):
-            fetch(1, LIST_ORDER[-1], first, first + T // 2)
-        for block in range(T // P):
-            cols = slice(block * P, (block + 1) * P)
-            result = keep.tile([P, P], F32, name="result%d" % block, align_bytes=ROW_ALIGN)
-            nc.vector.tensor_tensor(out=result[:], in0=prod[1][LIST_ORDER[-1]][:, cols], in1=block_bank[block][:, 0:P], op=ADD)
-            nc.sync.dma_start(out=out[P : 2 * P, cols], in_=result[:])
+        sum_banks = ((bank[2],), (bank[3], bank[4]))
+        fetch_raw(0, 0)
+        fetch_raw(1, 0)
+        fetch_raw(0, 1)
+        lists = (3, 2, 0)
+        for r in lists:
+            (times_gate if r == 0 else fetch_times_gate)(0, r)
+            add_turned(sum_banks[0], 0, r, lists)
+        lists = (3, 0, 2)
+        fetch_times_gate(1, 3, "raw0_0")
+        add_turned(sum_banks[1], 1, 3, lists)
+        times_gate(1, 0)
+        add_turned(sum_banks[1], 1, 0, lists)
+        turn_back(sum_banks[0], 0)
+        fetch_raw(1, 1, "prod0_0")
+        fetch_times_gate(1, 2, "raw1_0")
+        add_turned(sum_banks[1], 1, 2, lists)
+        turn_back(sum_banks[1], 1)
+        times_gate(0, 1, "gate_sb2")
+        times_gate(1, 1)
+        finish(sum_banks[0], 0, T, "raw1_1")
+        finish(sum_banks[1], 1, P)

@@ -32,7 +32,7 @@ ROW_ALIGN = 2048
 GATHER_GROUP = 2
 COPY = mybir.ActivationFunctionType.Copy
 LIST_LOADS = (0, 3, 2, 1)
-GATE_LOADS = (3, 2, 0, 1)
+GATE_LOADS = (3, 2, 1, 0)
 
 
 def load_scale_rows(queue, plane, rows):
@@ -61,7 +61,7 @@ def tile_moe_ecr_glu_sigmoid_kernel(
         w_sb = [[keep.tile([P, PASSES, 2 * H], U8, name="w_sb%d_%d" % (m, e), tag="w_sb%d_%d" % (m, e), align_bytes=ROW_ALIGN) for e in range(E)] for m in range(2)]
         w2_sb = keep.tile([P, E, 2 * N], U8, name="w2_sb", align_bytes=ROW_ALIGN)
         gate_sb = [keep.tile([P, T], F32, name="gate_sb%d" % r, tag="gate_sb%d" % r, align_bytes=ROW_ALIGN) for r in range(TOP)]
-        y_win = [keep.tile([P, SLOTS + PAD], F32, name="y_win%d" % hf, align_bytes=ALIGN) for hf in range(HALVES)]
+        y_win = [keep.tile([P, SLOTS + PAD], F32, name="y_win0", tag="y_win0", align_bytes=ROW_ALIGN)]
         ident = keep.tile([P, P], F32, name="ident", align_bytes=ALIGN)
 
         make_identity(nc, ident[:])
@@ -76,8 +76,7 @@ def tile_moe_ecr_glu_sigmoid_kernel(
 
         for plane in (late_plane[1], w2_plane):
             clear_one_port(plane)
-        for hf in range(HALVES):
-            nc.vector.memset(y_win[hf][:, SLOTS:], 0.0)
+        nc.vector.memset(y_win[0][:, SLOTS:], 0.0)
 
         w_all = [words.bitcast(I32).rearrange("e s p c -> p (e s) c") for words in (w1_words, w3_words)]
         w_rows = [scales.bitcast(I32).rearrange("e s (q r) c -> r q (e s) c", r=4) for scales in (w1_scales, w3_scales)]
@@ -216,12 +215,13 @@ def tile_moe_ecr_glu_sigmoid_kernel(
             (0, (2, 3), 4, nc.scalar.copy),
             (0, (4,), 1, nc.vector.tensor_copy),
             (0, (5,), 0, nc.scalar.copy),
-            (1, (0, 1, 2, 3), 7, nc.vector.tensor_copy),
+            (1, (0, 1, 2, 3), 5, nc.scalar.copy),
             (1, (4, 5), 6, nc.scalar.copy),
         )
         for hf, experts, b, move in shares:
             second_layer(hf, experts, bank[b])
-            keep_results(hf, experts, bank[b], move)
+            if hf == 0:
+                keep_results(hf, experts, bank[b], move)
 
         tiles = {}
 
@@ -229,17 +229,21 @@ def tile_moe_ecr_glu_sigmoid_kernel(
             tiles[name] = keep.tile([P, T], F32, name=name, tag=after or name, align_bytes=ROW_ALIGN)
             return tiles[name]
 
-        def fetch_times_gate(hf, r, after=None):
+        def fetch_times_gate(hf, r, after=None, piece=T):
             prod = row_tile("prod%d_%d" % (hf, r), after)
-            nc.vector.tensor_tensor(out=prod[:], in0=y_win[hf][:].indirect(pos_sb[r][:]), in1=gate_sb[r][:], op=MULT)
+            for col in range(0, T, piece):
+                picks = pos_sb[r][:, col // 16 : (col + piece) // 16]
+                nc.vector.tensor_tensor(out=prod[:, col : col + piece], in0=y_win[hf][:].indirect(picks), in1=gate_sb[r][:, col : col + piece], op=MULT)
 
         def fetch_raw(hf, r, after=None):
             raw = row_tile("raw%d_%d" % (hf, r), after)
             nc.scalar.activation(out=raw[:], in_=y_win[hf][:].indirect(pos_sb[r][:]), func=COPY)
 
-        def times_gate(hf, r, after=None):
+        def times_gate(hf, r, after=None, piece=T):
             prod = row_tile("prod%d_%d" % (hf, r), after)
-            nc.vector.tensor_tensor(out=prod[:], in0=tiles["raw%d_%d" % (hf, r)][:], in1=gate_sb[r][:], op=MULT)
+            for col in range(0, T, piece):
+                cols = slice(col, col + piece)
+                nc.vector.tensor_tensor(out=prod[:, cols], in0=tiles["raw%d_%d" % (hf, r)][:, cols], in1=gate_sb[r][:, cols], op=MULT)
 
         def add_turned(banks, hf, r, lists):
             share = T // len(banks)
@@ -261,33 +265,40 @@ def tile_moe_ecr_glu_sigmoid_kernel(
                 for col in range(0, share, P):
                     nc.tensor.transpose(held[:, col : col + P], summed[:, place * share + col : place * share + col + P], ident[:])
 
-        def finish(banks, hf, piece, after=None):
+        def finish(banks, hf, r, piece):
             share = T // len(banks)
-            result = row_tile("result%d" % hf, after)
+            result = row_tile("result%d" % hf)
             for col in range(0, T, piece):
                 cols = slice(col, col + piece)
-                nc.vector.tensor_tensor(out=result[:, cols], in0=tiles["prod%d_1" % hf][:, cols], in1=banks[col // share][:, col % share : col % share + piece], op=ADD)
+                nc.vector.tensor_tensor(out=result[:, cols], in0=tiles["prod%d_%d" % (hf, r)][:, cols], in1=banks[col // share][:, col % share : col % share + piece], op=ADD)
                 nc.sync.dma_start(out=out[hf * P : (hf + 1) * P, cols], in_=result[:, cols])
 
-        sum_banks = ((bank[2],), (bank[3], bank[4]))
+        sum_banks = ((bank[2], bank[7]), (bank[3], bank[4], bank[0], bank[1]))
         fetch_raw(0, 0)
-        fetch_raw(1, 0)
-        fetch_raw(0, 1)
-        lists = (3, 2, 0)
+        lists = (3, 2, 1, 0)
         for r in lists:
             (times_gate if r == 0 else fetch_times_gate)(0, r)
             add_turned(sum_banks[0], 0, r, lists)
-        lists = (3, 0, 2)
-        fetch_times_gate(1, 3, "raw0_0")
-        add_turned(sum_banks[1], 1, 3, lists)
-        times_gate(1, 0)
-        add_turned(sum_banks[1], 1, 0, lists)
+            if r == lists[0]:
+                y_win.append(keep.tile([P, SLOTS + PAD], F32, name="y_win1", tag="prod0_%d" % r, align_bytes=ROW_ALIGN))
+                nc.gpsimd.memset(y_win[1][:, SLOTS:], 0.0)
+                for hf, experts, b, move in shares:
+                    if hf == 1:
+                        keep_results(hf, experts, bank[b], move)
+                fetch_raw(1, 0)
         turn_back(sum_banks[0], 0)
-        fetch_raw(1, 1, "prod0_0")
-        fetch_times_gate(1, 2, "raw1_0")
+        first_half = row_tile("result0")
+        for pair in range(2):
+            nc.scalar.copy(out=first_half[:, pair * 2 * P : (pair + 1) * 2 * P], in_=sum_banks[0][pair][:, 0 : 2 * P])
+        nc.sync.dma_start(out=out[0:P, :], in_=first_half[:])
+
+        lists = (3, 2, 0)
+        fetch_times_gate(1, 3, "y_win0")
+        add_turned(sum_banks[1], 1, 3, lists)
+        fetch_times_gate(1, 2, "raw0_0")
         add_turned(sum_banks[1], 1, 2, lists)
+        times_gate(1, 0, None, P)
+        add_turned(sum_banks[1], 1, 0, lists)
         turn_back(sum_banks[1], 1)
-        times_gate(0, 1, "gate_sb2")
-        times_gate(1, 1)
-        finish(sum_banks[0], 0, T, "raw1_1")
-        finish(sum_banks[1], 1, P)
+        fetch_times_gate(1, 1, "gate_sb2", T // 2)
+        finish(sum_banks[1], 1, 1, P)

@@ -61,7 +61,7 @@ def tile_moe_ecr_glu_sigmoid_kernel(
         w_sb = [[keep.tile([P, PASSES, 2 * H], U8, name="w_sb%d_%d" % (m, e), tag="w_sb%d_%d" % (m, e), align_bytes=ROW_ALIGN) for e in range(E)] for m in range(2)]
         w2_sb = keep.tile([P, E, 2 * N], U8, name="w2_sb", align_bytes=ROW_ALIGN)
         gate_sb = [keep.tile([P, T], F32, name="gate_sb%d" % r, tag="gate_sb%d" % r, align_bytes=ROW_ALIGN) for r in range(TOP)]
-        y_win = [keep.tile([P, SLOTS + PAD], F32, name="y_win0", tag="y_win0", align_bytes=ROW_ALIGN)]
+        y_win = [keep.tile([P, SLOTS + PAD], F32, name="y_win%d" % hf, tag="y_win%d" % hf, align_bytes=ROW_ALIGN) for hf in range(HALVES)]
         ident = keep.tile([P, P], F32, name="ident", align_bytes=ALIGN)
 
         make_identity(nc, ident[:])
@@ -76,7 +76,8 @@ def tile_moe_ecr_glu_sigmoid_kernel(
 
         for plane in (late_plane[1], w2_plane):
             clear_one_port(plane)
-        nc.vector.memset(y_win[0][:, SLOTS:], 0.0)
+        for hf in range(HALVES):
+            nc.vector.memset(y_win[hf][:, SLOTS:], 0.0)
 
         w_all = [words.bitcast(I32).rearrange("e s p c -> p (e s) c") for words in (w1_words, w3_words)]
         w_rows = [scales.bitcast(I32).rearrange("e s (q r) c -> r q (e s) c", r=4) for scales in (w1_scales, w3_scales)]
@@ -214,14 +215,13 @@ def tile_moe_ecr_glu_sigmoid_kernel(
             (0, (0, 1), 3, nc.scalar.copy),
             (0, (2, 3), 4, nc.scalar.copy),
             (0, (4,), 1, nc.vector.tensor_copy),
+            (1, (0, 1, 2), 7, nc.vector.tensor_copy),
             (0, (5,), 0, nc.scalar.copy),
-            (1, (0, 1, 2, 3), 5, nc.scalar.copy),
-            (1, (4, 5), 6, nc.scalar.copy),
+            (1, (3, 4, 5), 6, nc.scalar.copy),
         )
         for hf, experts, b, move in shares:
             second_layer(hf, experts, bank[b])
-            if hf == 0:
-                keep_results(hf, experts, bank[b], move)
+            keep_results(hf, experts, bank[b], move)
 
         tiles = {}
 
@@ -273,19 +273,13 @@ def tile_moe_ecr_glu_sigmoid_kernel(
                 nc.vector.tensor_tensor(out=result[:, cols], in0=tiles["prod%d_%d" % (hf, r)][:, cols], in1=banks[col // share][:, col % share : col % share + piece], op=ADD)
                 nc.sync.dma_start(out=out[hf * P : (hf + 1) * P, cols], in_=result[:, cols])
 
-        sum_banks = ((bank[2], bank[7]), (bank[3], bank[4], bank[0], bank[1]))
+        sum_banks = ((bank[2], bank[5]), (bank[3], bank[4], bank[0], bank[1]))
         fetch_raw(0, 0)
+        fetch_raw(1, 0)
         lists = (3, 2, 1, 0)
         for r in lists:
             (times_gate if r == 0 else fetch_times_gate)(0, r)
             add_turned(sum_banks[0], 0, r, lists)
-            if r == lists[0]:
-                y_win.append(keep.tile([P, SLOTS + PAD], F32, name="y_win1", tag="prod0_%d" % r, align_bytes=ROW_ALIGN))
-                nc.gpsimd.memset(y_win[1][:, SLOTS:], 0.0)
-                for hf, experts, b, move in shares:
-                    if hf == 1:
-                        keep_results(hf, experts, bank[b], move)
-                fetch_raw(1, 0)
         turn_back(sum_banks[0], 0)
         first_half = row_tile("result0")
         for pair in range(2):

@@ -32,7 +32,6 @@ ROW_ALIGN = 2048
 GATHER_GROUP = 2
 COPY = mybir.ActivationFunctionType.Copy
 LIST_LOADS = (0, 3, 2, 1)
-GATE_LOADS = (3, 2, 1, 0)
 
 
 def load_scale_rows(queue, plane, rows):
@@ -60,7 +59,8 @@ def tile_moe_ecr_glu_sigmoid_kernel(
         w2_plane = keep.tile([P, E, N], U8, name="w2_plane", align_bytes=ROW_ALIGN)
         w_sb = [[keep.tile([P, PASSES, 2 * H], U8, name="w_sb%d_%d" % (m, e), tag="w_sb%d_%d" % (m, e), align_bytes=ROW_ALIGN) for e in range(E)] for m in range(2)]
         w2_sb = keep.tile([P, E, 2 * N], U8, name="w2_sb", align_bytes=ROW_ALIGN)
-        gate_sb = [keep.tile([P, T], F32, name="gate_sb%d" % r, tag="gate_sb%d" % r, align_bytes=ROW_ALIGN) for r in range(TOP)]
+        gate_pair = keep.tile([P, 2, T], F32, name="gate_pair", align_bytes=ROW_ALIGN)
+        gate_sb = [gate_pair[:, r, :] for r in range(2)] + [keep.tile([P, T], F32, name="gate_sb%d" % r, tag="gate_sb%d" % r, align_bytes=ROW_ALIGN)[:] for r in range(2, TOP)]
         y_win = [keep.tile([P, SLOTS + PAD], F32, name="y_win%d" % hf, tag="y_win%d" % hf, align_bytes=ROW_ALIGN) for hf in range(HALVES)]
         ident = keep.tile([P, P], F32, name="ident", align_bytes=ALIGN)
 
@@ -97,13 +97,18 @@ def tile_moe_ecr_glu_sigmoid_kernel(
         load_scale_rows(nc.sync, late_plane[1], w_rows[1][:, :, EARLY[1] * PASSES :, :])
         for e in range(1, E):
             for m in (1, 0) if e == EARLY[0] else (0, 1):
-                load_words(m, e)
+                if (m, e) == (1, LAST):
+                    for s in range(PASSES):
+                        load_words(m, e, s, s + 1)
+                else:
+                    load_words(m, e)
         load_scale_rows(nc.sync, w2_plane, w2_scales.bitcast(I32).rearrange("e s (q r) c -> r q (e s) c", r=4))
         nc.sync.dma_start(out=w2_sb[:].bitcast(I32), in_=w2_all)
         for r in LIST_LOADS:
             nc.sync.dma_start(pos_sb[r][:], (pos1, pos2, pos3, pos4)[r])
-        for r in GATE_LOADS:
-            nc.sync.dma_start(out=gate_sb[r][:], in_=gate[r, 0:P, :])
+        for r in (3, 2):
+            nc.sync.dma_start(out=gate_sb[r], in_=gate[r, 0:P, :])
+        nc.sync.dma_start(out=gate_pair[:], in_=gate[0:2, 0:P, :].rearrange("r p t -> p r t"))
 
         width = GATHER_GROUP * C
         x_slot = {}
@@ -215,9 +220,9 @@ def tile_moe_ecr_glu_sigmoid_kernel(
             (0, (0, 1), 3, nc.scalar.copy),
             (0, (2, 3), 4, nc.scalar.copy),
             (0, (4,), 1, nc.vector.tensor_copy),
-            (1, (0, 1, 2), 7, nc.vector.tensor_copy),
+            (1, (0, 1), 7, nc.vector.tensor_copy),
             (0, (5,), 0, nc.scalar.copy),
-            (1, (3, 4, 5), 6, nc.scalar.copy),
+            (1, (2, 3, 4, 5), 6, nc.scalar.copy),
         )
         for hf, experts, b, move in shares:
             second_layer(hf, experts, bank[b])
@@ -278,7 +283,7 @@ def tile_moe_ecr_glu_sigmoid_kernel(
         fetch_raw(1, 0)
         lists = (3, 2, 1, 0)
         for r in lists:
-            (times_gate if r == 0 else fetch_times_gate)(0, r)
+            (times_gate if r == 0 else fetch_times_gate)(0, r, None, T if r > 1 else T // 2)
             add_turned(sum_banks[0], 0, r, lists)
         turn_back(sum_banks[0], 0)
         first_half = row_tile("result0")
@@ -287,9 +292,9 @@ def tile_moe_ecr_glu_sigmoid_kernel(
         nc.sync.dma_start(out=out[0:P, :], in_=first_half[:])
 
         lists = (3, 2, 0)
-        fetch_times_gate(1, 3, "y_win0")
+        fetch_times_gate(1, 3, "y_win0", T // 2)
         add_turned(sum_banks[1], 1, 3, lists)
-        fetch_times_gate(1, 2, "raw0_0")
+        fetch_times_gate(1, 2, "raw0_0", T // 2)
         add_turned(sum_banks[1], 1, 2, lists)
         times_gate(1, 0, None, P)
         add_turned(sum_banks[1], 1, 0, lists)

@@ -124,40 +124,42 @@ def tile_moe_ecr_glu_sigmoid_kernel(
             for s in range(PASSES):
                 nc.vector.tensor_copy(out=xs_slot[g][s][:], in_=xs_win[:, s, :].indirect(picks))
 
-        def first_product(m, e):
+        def first_product(m, e, banks):
             g, place = divmod(e, GATHER_GROUP)
-            cols = slice(place * C, (place + 1) * C)
-            acc = bank[3 * m + e % 3]
+            slots = slice(place * C, (place + 1) * C)
+            share = H // len(banks)
             for s in range(PASSES):
                 plane = early_plane[m][:, e * PASSES + s, :] if e < EARLY[m] else late_plane[m][:, (e - EARLY[m]) * PASSES + s, :]
-                nc.tensor.matmul_mx(
-                    out=acc[:],
-                    lhsT=x_slot[g][s][:, cols].bitcast(FP8X4),
-                    lhsT_scale=xs_slot[g][s][:, cols],
-                    rhs=w_sb[m][e][:, s, :].bitcast(FP4X4),
-                    rhs_scale=plane,
-                    start=(s == 0),
-                    stop=(s == PASSES - 1),
-                )
-            return acc[:].rearrange("j (p u d) -> j u p d", u=2, d=2)
-
-        def by_halves(e):
-            return (slice(0, 1), slice(1, 2)) if e == LAST else (slice(0, 2),)
+                for part, acc in enumerate(banks):
+                    nc.tensor.matmul_mx(
+                        out=acc[:, 0:share],
+                        lhsT=x_slot[g][s][:, slots].bitcast(FP8X4),
+                        lhsT_scale=xs_slot[g][s][:, slots],
+                        rhs=w_sb[m][e][:, s, 2 * part * share : 2 * (part + 1) * share].bitcast(FP4X4),
+                        rhs_scale=plane[:, part * share : (part + 1) * share],
+                        start=(s == 0),
+                        stop=(s == PASSES - 1),
+                    )
+            return [acc[:, 0:share].rearrange("j (p u d) -> j u p d", u=2, d=2) for acc in banks]
 
         def first_layer(e):
-            a_sum = first_product(0, e)
-            b_sum = first_product(1, e)
+            a_sum = first_product(0, e, [bank[e % 3]])[0]
+            b_sums = first_product(1, e, [bank[5], bank[3]] if e == LAST else [bank[3 + e % 3]])
             sig = keep.tile([C, 2, P, 2], F32, name="sig%d" % e, tag="sig%d" % e, align_bytes=ALIGN)
-            for us in by_halves(e):
-                nc.scalar.activation(out=sig[:, us], in_=a_sum[:, us], func=SIGMOID)
-            return sig, b_sum
+            share = P // len(b_sums)
+            for part in range(len(b_sums)):
+                ps = slice(part * share, (part + 1) * share)
+                nc.scalar.activation(out=sig[:, :, ps, :], in_=a_sum[:, :, ps, :], func=SIGMOID)
+            return sig, b_sums
 
         h_rows = {}
 
-        def gated_product(e, sig, b_sum):
+        def gated_product(e, sig, b_sums):
             h_rows[e] = keep.tile([C, 2, P, 2], BF16, name="h_rows%d" % e, align_bytes=ALIGN)
-            for us in by_halves(e):
-                nc.vector.tensor_tensor(out=h_rows[e][:, us], in0=sig[:, us], in1=b_sum[:, us], op=MULT)
+            share = P // len(b_sums)
+            for part, b_sum in enumerate(b_sums):
+                ps = slice(part * share, (part + 1) * share)
+                nc.vector.tensor_tensor(out=h_rows[e][:, :, ps, :], in0=sig[:, :, ps, :], in1=b_sum, op=MULT)
 
         h_codes = {}
         h_scales = {}
@@ -264,11 +266,12 @@ def tile_moe_ecr_glu_sigmoid_kernel(
 
         def turn_back(banks, hf):
             share = T // len(banks)
-            summed = row_tile("sum%d" % hf)
             for place, held in enumerate(banks):
-                nc.scalar.copy(out=summed[:, place * share : (place + 1) * share], in_=held[:, 0:share])
+                summed = keep.tile([P, share], F32, name="sum%d_%d" % (hf, place), align_bytes=ALIGN)
+                tiles["sum%d_%d" % (hf, place)] = summed
+                nc.scalar.copy(out=summed[:], in_=held[:, 0:share])
                 for col in range(0, share, P):
-                    nc.tensor.transpose(held[:, col : col + P], summed[:, place * share + col : place * share + col + P], ident[:])
+                    nc.tensor.transpose(held[:, col : col + P], summed[:, col : col + P], ident[:])
 
         def finish(banks, hf, r, piece):
             share = T // len(banks)

@@ -31,7 +31,6 @@ ALIGN = 256
 ROW_ALIGN = 2048
 GATHER_GROUP = 2
 COPY = mybir.ActivationFunctionType.Copy
-LIST_LOADS = (0, 3, 2, 1)
 
 
 def load_scale_rows(queue, plane, rows):
@@ -56,9 +55,9 @@ def tile_moe_ecr_glu_sigmoid_kernel(
         xs_win = keep.tile([P, PASSES, T], U8, name="xs_win", align_bytes=ROW_ALIGN)
         early_plane = [keep.tile([P, EARLY[m] * PASSES, H], U8, name="early_plane%d" % m, align_bytes=ROW_ALIGN) for m in range(2)]
         late_plane = [keep.tile([P, (E - EARLY[m]) * PASSES, H], U8, name="late_plane%d" % m, align_bytes=ROW_ALIGN) for m in range(2)]
-        w2_plane = keep.tile([P, E, N], U8, name="w2_plane", align_bytes=ROW_ALIGN)
+        w2_plane = keep.tile([P, E, 2 * N], U8, name="w2_plane", align_bytes=ROW_ALIGN)[:, :, 0:N]
         w_sb = [[keep.tile([P, PASSES, 2 * H], U8, name="w_sb%d_%d" % (m, e), tag="w_sb%d_%d" % (m, e), align_bytes=ROW_ALIGN) for e in range(E)] for m in range(2)]
-        w2_sb = keep.tile([P, E, 2 * N], U8, name="w2_sb", align_bytes=ROW_ALIGN)
+        w2_sb = keep.tile([P, E, 3 * N], U8, name="w2_sb", align_bytes=ROW_ALIGN)[:, :, 0 : 2 * N]
         gate_pair = keep.tile([P, 2, T], F32, name="gate_pair", align_bytes=ROW_ALIGN)
         gate_sb = [gate_pair[:, r, :] for r in range(2)] + [keep.tile([P, T], F32, name="gate_sb%d" % r, tag="gate_sb%d" % r, align_bytes=ROW_ALIGN)[:] for r in range(2, TOP)]
         y_win = [keep.tile([P, SLOTS + PAD], F32, name="y_win%d" % hf, tag="y_win%d" % hf, align_bytes=ROW_ALIGN) for hf in range(HALVES)]
@@ -74,8 +73,9 @@ def tile_moe_ecr_glu_sigmoid_kernel(
             nc.vector.memset(words[:, 0 : count - 1], 0)
             nc.vector.memset(words[:, count - 1 : count], 0)
 
-        for plane in (late_plane[1], w2_plane):
-            clear_one_port(plane)
+        clear_one_port(late_plane[1])
+        nc.vector.memset(w2_plane[:, 0:LAST, :].bitcast(I32), 0)
+        nc.vector.memset(w2_plane[:, LAST, :].bitcast(I32), 0)
         for hf in range(HALVES):
             nc.vector.memset(y_win[hf][:, SLOTS:], 0.0)
 
@@ -103,11 +103,14 @@ def tile_moe_ecr_glu_sigmoid_kernel(
                 else:
                     load_words(m, e)
         load_scale_rows(nc.sync, w2_plane, w2_scales.bitcast(I32).rearrange("e s (q r) c -> r q (e s) c", r=4))
-        nc.sync.dma_start(out=w2_sb[:].bitcast(I32), in_=w2_all)
-        for r in LIST_LOADS:
-            nc.sync.dma_start(pos_sb[r][:], (pos1, pos2, pos3, pos4)[r])
-        for r in (3, 2):
-            nc.sync.dma_start(out=gate_sb[r], in_=gate[r, 0:P, :])
+        nc.sync.dma_start(out=w2_sb.bitcast(I32), in_=w2_all)
+        pos = (pos1, pos2, pos3, pos4)
+        nc.sync.dma_start(pos_sb[3][:], pos[3])
+        nc.sync.dma_start(out=gate_sb[3], in_=gate[3, 0:P, :])
+        for r in (0, 2):
+            nc.sync.dma_start(pos_sb[r][:], pos[r])
+        nc.sync.dma_start(out=gate_sb[2], in_=gate[2, 0:P, :])
+        nc.sync.dma_start(pos_sb[1][:], pos[1])
         nc.sync.dma_start(out=gate_pair[:], in_=gate[0:2, 0:P, :].rearrange("r p t -> p r t"))
 
         width = GATHER_GROUP * C

from contextlib import ExitStack

import concourse.mybir as mybir
from concourse.masks import make_identity

K, T, E, C, H, N = 1024, 512, 6, 128, 512, 256
TOP = 4
PAD = 64
SLOTS = E * C
P = 128
PASSES = K // 512
HALVES = N // P
LAST = E - 1

FLOPS = 2 * SLOTS * (2 * K * H + H * N)

F32 = mybir.dt.float32
BF16 = mybir.dt.bfloat16
I32 = mybir.dt.int32
U32 = mybir.dt.uint32
U16 = mybir.dt.uint16
U8 = mybir.dt.uint8
FP8X4 = mybir.dt.float8_e4m3fn_x4
FP4X4 = mybir.dt.float4_e2m1fn_x4
MULT = mybir.AluOpType.mult
ADD = mybir.AluOpType.add
SIGMOID = mybir.ActivationFunctionType.Sigmoid

EARLY = (2, 2)
ALIGN = 256
ROW_ALIGN = 2048
GATHER_GROUP = 2
COPY = mybir.ActivationFunctionType.Copy


def load_scale_rows(queue, plane, rows):
    for r in range(4):
        queue.dma_start(out=plane[r:P:32, :, :].bitcast(I32), in_=rows[r])


def tile_moe_ecr_glu_sigmoid_kernel(
    tc, x_words, x_scales, w1_words, w1_scales, w3_words, w3_scales, w2_words, w2_scales, gate, offs, pos1, pos2, pos3, pos4, out
):
    nc = tc.nc
    with ExitStack() as ctx:
        lists = ctx.enter_context(tc.tile_pool(name="lists", bufs=1))
        keep = ctx.enter_context(tc.tile_pool(name="keep", bufs=1))
        psum = ctx.enter_context(tc.psum_pool(name="psum", bufs=1))
        bank = [psum.tile([P, 512], F32, name="bank%d" % b) for b in range(8)]

        offs_sb = lists.tile([P, SLOTS // 16], U16, name="offs_sb")
        pos_sb = [lists.tile([P, T // 16], U16, name="pos_sb%d" % r) for r in range(TOP)]

        x_win = keep.tile([P, PASSES, T], I32, name="x_win", align_bytes=ROW_ALIGN)
        xs_win = keep.tile([P, PASSES, T], U8, name="xs_win", align_bytes=ROW_ALIGN)
        early_plane = [keep.tile([P, EARLY[m] * PASSES, H], U8, name="early_plane%d" % m, align_bytes=ROW_ALIGN) for m in range(2)]
        late_plane = [keep.tile([P, (E - EARLY[m]) * PASSES, H], U8, name="late_plane%d" % m, align_bytes=ROW_ALIGN) for m in range(2)]
        w2_plane = keep.tile([P, E, 2 * N], U8, name="w2_plane", align_bytes=ROW_ALIGN)[:, :, 0:N]
        w_sb = [[keep.tile([P, PASSES, 2 * H], U8, name="w_sb%d_%d" % (m, e), tag="w_sb%d_%d" % (m, e), align_bytes=ROW_ALIGN) for e in range(E)] for m in range(2)]
        w2_sb = keep.tile([P, E, 3 * N], U8, name="w2_sb", align_bytes=ROW_ALIGN)[:, :, 0 : 2 * N]
        gate_pair = keep.tile([P, 2, T], F32, name="gate_pair", align_bytes=ROW_ALIGN)
        gate_sb = [gate_pair[:, r, :] for r in range(2)] + [keep.tile([P, T], F32, name="gate_sb%d" % r, tag="gate_sb%d" % r, align_bytes=ROW_ALIGN)[:] for r in range(2, TOP)]
        y_win = [keep.tile([P, SLOTS + PAD], F32, name="y_win%d" % hf, tag="y_win%d" % hf, align_bytes=ROW_ALIGN) for hf in range(HALVES)]
        ident = keep.tile([P, P], F32, name="ident", align_bytes=ALIGN)

        make_identity(nc, ident[:])
        for plane in (xs_win, early_plane[0], early_plane[1], late_plane[0]):
            nc.vector.memset(plane[:].bitcast(I32), 0)

        def clear_one_port(plane):
            words = plane[:].rearrange("p a c -> p (a c)").bitcast(I32)
            count = words.shape[1]
            nc.vector.memset(words[:, 0 : count - 1], 0)
            nc.vector.memset(words[:, count - 1 : count], 0)

        clear_one_port(late_plane[1])
        nc.vector.memset(w2_plane[:, 0:LAST, :].bitcast(I32), 0)
        nc.vector.memset(w2_plane[:, LAST, :].bitcast(I32), 0)
        for hf in range(HALVES):
            nc.vector.memset(y_win[hf][:, SLOTS:], 0.0)

        w_all = [words.bitcast(I32).rearrange("e s p c -> p (e s) c") for words in (w1_words, w3_words)]
        w_rows = [scales.bitcast(I32).rearrange("e s (q r) c -> r q (e s) c", r=4) for scales in (w1_scales, w3_scales)]
        w2_all = w2_words.bitcast(I32).rearrange("e s p c -> p (e s) c")

        def load_words(m, e, first=0, last=PASSES):
            nc.sync.dma_start(out=w_sb[m][e][:, first:last, :].bitcast(I32), in_=w_all[m][:, e * PASSES + first : e * PASSES + last, :])

        nc.sync.dma_start(out=x_win[:], in_=x_words.rearrange("s p t r -> p s (t r)").bitcast(I32))
        load_scale_rows(nc.sync, xs_win, x_scales.bitcast(I32).rearrange("s (q r) c -> r q s c", r=4))
        nc.sync.dma_start(offs_sb[:], offs)
        load_scale_rows(nc.gpsimd, late_plane[0], w_rows[0][:, :, EARLY[0] * PASSES :, :])
        for m in range(2):
            load_words(m, 0)
        for m in range(2):
            load_scale_rows(nc.sync, early_plane[m], w_rows[m][:, :, 0 : EARLY[m] * PASSES, :])
        load_scale_rows(nc.sync, late_plane[1], w_rows[1][:, :, EARLY[1] * PASSES :, :])
        for e in range(1, E):
            for m in (1, 0) if e == EARLY[0] else (0, 1):
                if (m, e) == (1, LAST):
                    for s in range(PASSES):
                        load_words(m, e, s, s + 1)
                else:
                    load_words(m, e)
        load_scale_rows(nc.sync, w2_plane, w2_scales.bitcast(I32).rearrange("e s (q r) c -> r q (e s) c", r=4))
        nc.sync.dma_start(out=w2_sb.bitcast(I32), in_=w2_all)
        pos = (pos1, pos2, pos3, pos4)
        nc.sync.dma_start(pos_sb[3][:], pos[3])
        nc.sync.dma_start(out=gate_sb[3], in_=gate[3, 0:P, :])
        for r in (0, 2):
            nc.sync.dma_start(pos_sb[r][:], pos[r])
        nc.sync.dma_start(out=gate_sb[2], in_=gate[2, 0:P, :])
        nc.sync.dma_start(pos_sb[1][:], pos[1])
        nc.sync.dma_start(out=gate_pair[:], in_=gate[0:2, 0:P, :].rearrange("r p t -> p r t"))

        width = GATHER_GROUP * C
        x_slot = {}
        xs_slot = {}

        def gather_tokens(g):
            picks = offs_sb[:, g * width // 16 : (g + 1) * width // 16]
            last = g == E // GATHER_GROUP - 1
            x_slot[g] = [keep.tile([P, width], U32, name="x_slot%d_%d" % (g, s), align_bytes=ALIGN) for s in range(PASSES)]
            xs_slot[g] = [keep.tile([P, width], U8, name="xs_slot%d_%d" % (g, s), tag="sig%d" % s if last else "xs_slot%d_%d" % (g, s), align_bytes=ALIGN) for s in range(PASSES)]
            for s in range(PASSES):
                nc.vector.tensor_copy(out=x_slot[g][s][:], in_=x_win[:, s, :].bitcast(U32).indirect(picks))
            for s in range(PASSES):
                nc.vector.tensor_copy(out=xs_slot[g][s][:], in_=xs_win[:, s, :].indirect(picks))

        def first_product(m, e, banks):
            g, place = divmod(e, GATHER_GROUP)
            slots = slice(place * C, (place + 1) * C)
            share = H // len(banks)
            for s in range(PASSES):
                plane = early_plane[m][:, e * PASSES + s, :] if e < EARLY[m] else late_plane[m][:, (e - EARLY[m]) * PASSES + s, :]
                for part, acc in enumerate(banks):
                    nc.tensor.matmul_mx(
                        out=acc[:, 0:share],
                        lhsT=x_slot[g][s][:, slots].bitcast(FP8X4),
                        lhsT_scale=xs_slot[g][s][:, slots],
                        rhs=w_sb[m][e][:, s, 2 * part * share : 2 * (part + 1) * share].bitcast(FP4X4),
                        rhs_scale=plane[:, part * share : (part + 1) * share],
                        start=(s == 0),
                        stop=(s == PASSES - 1),
                    )
            return [acc[:, 0:share].rearrange("j (p u d) -> j u p d", u=2, d=2) for acc in banks]

        def first_layer(e):
            a_sum = first_product(0, e, [bank[e % 3]])[0]
            b_sums = first_product(1, e, [bank[5], bank[3]] if e == LAST else [bank[3 + e % 3]])
            sig = keep.tile([C, 2, P, 2], F32, name="sig%d" % e, tag="sig%d" % e, align_bytes=ALIGN)
            share = P // len(b_sums)
            for part in range(len(b_sums)):
                ps = slice(part * share, (part + 1) * share)
                nc.scalar.activation(out=sig[:, :, ps, :], in_=a_sum[:, :, ps, :], func=SIGMOID)
            return sig, b_sums

        h_rows = {}

        def gated_product(e, sig, b_sums):
            h_rows[e] = keep.tile([C, 2, P, 2], BF16, name="h_rows%d" % e, align_bytes=ALIGN)
            share = P // len(b_sums)
            for part, b_sum in enumerate(b_sums):
                ps = slice(part * share, (part + 1) * share)
                nc.vector.tensor_tensor(out=h_rows[e][:, :, ps, :], in0=sig[:, :, ps, :], in1=b_sum, op=MULT)

        h_codes = {}
        h_scales = {}

        h_cols = {}

        def turn(experts, into, move):
            count = len(experts)
            turned = into[:, 0 : count * 2 * C].rearrange("p (e u j) -> p e u j", u=2, j=C)
            for place, e in enumerate(experts):
                pairs = h_rows[e][:].rearrange("j u p d -> j (u p d)").bitcast(F32)
                for u in range(2):
                    nc.tensor.transpose(turned[:, place, u, :], pairs[:, u * P : (u + 1) * P], ident[:])
            h_cols[experts] = keep.tile([P, count * 4 * C], BF16, name="h_cols%d" % experts[0], align_bytes=ALIGN)
            move(out=h_cols[experts][:].bitcast(F32).rearrange("p (e j u) -> p e j u", u=2, j=C), in_=turned.rearrange("p e u j -> p e j u"))

        def quantize(experts):
            count = len(experts)
            codes = keep.tile([P, count * C], U32, name="h_codes%d" % experts[0], tag=("sig2" if count == 2 else "h_codes%d" % experts[0]), align_bytes=ALIGN)
            scales = keep.tile([P, count * C], U8, name="h_scales%d" % experts[0], align_bytes=ALIGN)
            nc.vector.quantize_mx(out=codes[:].bitcast(FP8X4), scales=scales[:], in_=h_cols[experts][:])
            for place, e in enumerate(experts):
                h_codes[e] = codes[:, place * C : (place + 1) * C]
                h_scales[e] = scales[:, place * C : (place + 1) * C]

        def second_layer(hf, experts, y_acc):
            for place, e in enumerate(experts):
                nc.tensor.matmul_mx(
                    out=y_acc[:, place * C : (place + 1) * C],
                    lhsT=w2_sb[:, e, 2 * hf * P : 2 * (hf + 1) * P].bitcast(FP4X4),
                    lhsT_scale=w2_plane[:, e, hf * P : (hf + 1) * P],
                    rhs=h_codes[e].bitcast(FP8X4),
                    rhs_scale=h_scales[e],
                    start=True,
                    stop=True,
                )

        def keep_results(hf, experts, y_acc, move):
            move(out=y_win[hf][:, experts[0] * C : (experts[-1] + 1) * C], in_=y_acc[:, 0 : len(experts) * C])

        gather_tokens(0)
        gather_tokens(1)
        parts = {}
        for e in range(E + 1):
            if e < E:
                parts[e] = first_layer(e)
            if e > 0:
                gated_product(e - 1, *parts[e - 1])
            if e == 2:
                gather_tokens(2)
            if e == 3:
                turn((0, 1), bank[2], nc.scalar.copy)
                quantize((0, 1))
        late_turns = ((2, 4, nc.scalar.copy), (4, 6, nc.vector.tensor_copy), (3, 2, nc.scalar.copy), (5, 7, nc.scalar.copy))
        for e, b, move in late_turns:
            turn((e,), bank[b], move)
        for e, b, move in late_turns:
            quantize((e,))
        shares = (
            (0, (0, 1), 3, nc.scalar.copy),
            (0, (2, 3), 4, nc.scalar.copy),
            (0, (4,), 1, nc.vector.tensor_copy),
            (1, (0, 1), 7, nc.vector.tensor_copy),
            (0, (5,), 0, nc.scalar.copy),
            (1, (2, 3, 4, 5), 6, nc.scalar.copy),
        )
        for hf, experts, b, move in shares:
            second_layer(hf, experts, bank[b])
            keep_results(hf, experts, bank[b], move)

        tiles = {}

        def row_tile(name, after=None):
            tiles[name] = keep.tile([P, T], F32, name=name, tag=after or name, align_bytes=ROW_ALIGN)
            return tiles[name]

        def fetch_times_gate(hf, r, after=None, piece=T):
            prod = row_tile("prod%d_%d" % (hf, r), after)
            for col in range(0, T, piece):
                picks = pos_sb[r][:, col // 16 : (col + piece) // 16]
                nc.vector.tensor_tensor(out=prod[:, col : col + piece], in0=y_win[hf][:].indirect(picks), in1=gate_sb[r][:, col : col + piece], op=MULT)

        def fetch_raw(hf, r, after=None):
            raw = row_tile("raw%d_%d" % (hf, r), after)
            nc.scalar.activation(out=raw[:], in_=y_win[hf][:].indirect(pos_sb[r][:]), func=COPY)

        def times_gate(hf, r, after=None, piece=T):
            prod = row_tile("prod%d_%d" % (hf, r), after)
            for col in range(0, T, piece):
                cols = slice(col, col + piece)
                nc.vector.tensor_tensor(out=prod[:, cols], in0=tiles["raw%d_%d" % (hf, r)][:, cols], in1=gate_sb[r][:, cols], op=MULT)

        def add_turned(banks, hf, r, lists):
            share = T // len(banks)
            for col in range(0, T, P):
                nc.tensor.matmul(
                    banks[col // share][:, col % share : col % share + P],
                    lhsT=tiles["prod%d_%d" % (hf, r)][:, col : col + P],
                    rhs=ident[:],
                    is_transpose=True,
                    start=(r == lists[0] and col % share == 0),
                    stop=(r == lists[-1] and col % share == share - P),
                )

        def turn_back(banks, hf):
            share = T // len(banks)
            for place, held in enumerate(banks):
                summed = keep.tile([P, share], F32, name="sum%d_%d" % (hf, place), align_bytes=ALIGN)
                tiles["sum%d_%d" % (hf, place)] = summed
                nc.scalar.copy(out=summed[:], in_=held[:, 0:share])
                for col in range(0, share, P):
                    nc.tensor.transpose(held[:, col : col + P], summed[:, col : col + P], ident[:])

        def finish(banks, hf, r, piece):
            share = T // len(banks)
            result = row_tile("result%d" % hf)
            for col in range(0, T, piece):
                cols = slice(col, col + piece)
                nc.vector.tensor_tensor(out=result[:, cols], in0=tiles["prod%d_%d" % (hf, r)][:, cols], in1=banks[col // share][:, col % share : col % share + piece], op=ADD)
                nc.sync.dma_start(out=out[hf * P : (hf + 1) * P, cols], in_=result[:, cols])

        sum_banks = ((bank[2], bank[5]), (bank[3], bank[4], bank[0], bank[1]))
        fetch_raw(0, 0)
        fetch_raw(1, 0)
        lists = (3, 2, 1, 0)
        for r in lists:
            (times_gate if r == 0 else fetch_times_gate)(0, r, None, T if r > 1 else T // 2)
            add_turned(sum_banks[0], 0, r, lists)
        turn_back(sum_banks[0], 0)
        first_half = row_tile("result0")
        for pair in range(2):
            nc.scalar.copy(out=first_half[:, pair * 2 * P : (pair + 1) * 2 * P], in_=sum_banks[0][pair][:, 0 : 2 * P])
        nc.sync.dma_start(out=out[0:P, :], in_=first_half[:])

        lists = (3, 2, 0)
        fetch_times_gate(1, 3, "y_win0", T // 2)
        add_turned(sum_banks[1], 1, 3, lists)
        fetch_times_gate(1, 2, "raw0_0", T // 2)
        add_turned(sum_banks[1], 1, 2, lists)
        times_gate(1, 0, None, P)
        add_turned(sum_banks[1], 1, 0, lists)
        turn_back(sum_banks[1], 1)
        fetch_times_gate(1, 1, "gate_sb2", T // 2)
        finish(sum_banks[1], 1, 1, P)
